import numpy as np
import ml_dtypes


def mxq(x, axis, fmt="e4m3"):
    dtype, down = {"e4m3": (ml_dtypes.float8_e4m3fn, 7), "e5m2": (ml_dtypes.float8_e5m2, 14)}[fmt]
    v = np.moveaxis(np.asarray(x, np.float32).astype(ml_dtypes.bfloat16).astype(np.float64), axis, -1)
    blocks = v.reshape(v.shape[:-1] + (-1, 32))
    amax = np.abs(blocks).max(-1, keepdims=True)
    byte = np.maximum(np.where(amax > 0, np.frexp(amax)[1] - 1 + 127, 0) - down, 1)
    scale = np.exp2(byte - 127.0)
    codes = (blocks / scale).astype(np.float32).astype(dtype).astype(np.float64)
    return np.moveaxis((codes * scale).reshape(v.shape), -1, axis)


WIDE = False


def mx_kscale(k):
    if not WIDE:
        return np.ones(k)
    levels = np.array([10, -10, 5, -5, 0])
    if k % 512:
        return np.exp2(np.random.permutation(np.resize(levels, k // 32))).repeat(32)
    a = np.empty((k // 512, 16))
    for p in range(k // 512):
        a[p, :8] = np.random.permutation(np.resize(levels, 8))
        for g in range(8):
            far = levels[np.abs(levels - a[p, g]) >= 10]
            a[p, g + 8] = far[np.random.randint(len(far))]
    return np.exp2(a.ravel()).repeat(32)


def f64(x):
    return np.asarray(x).astype(np.float64)


def striped(idx):
    return np.tile(idx.reshape(-1, 16).T, (8, 1)).astype(np.uint16)


def unstriped(offs):
    return offs[:16].T.reshape(-1).astype(np.int64)


E2M1 = np.array([0.0, 0.5, 1.0, 1.5, 2.0, 3.0, 4.0, 6.0, -0.0, -0.5, -1.0, -1.5, -2.0, -3.0, -4.0, -6.0])


def pack_weight(w, fmt):
    k, n = w.shape
    w = f64(np.asarray(w, np.float32).astype(ml_dtypes.bfloat16)).reshape(k // 32, 32, n)
    amax = np.abs(w).max(1)
    if fmt == "e4m3":
        byte = np.frexp(amax)[1] - 1 + 127 - 7
    else:
        mant, ex = np.frexp(amax / 6.0)
        byte = np.where(mant > 0.5, ex, ex - 1) + 127
    byte = np.clip(np.where(amax > 0, byte, 1), 1, 254)
    scaled = (w * np.exp2(127.0 - byte)[:, None, :]).reshape(k, n).astype(np.float32)
    by_word = np.ascontiguousarray(scaled.reshape(k // 512, 128, 4, n).transpose(0, 1, 3, 2))
    if fmt == "e4m3":
        words = by_word.astype(ml_dtypes.float8_e4m3fn).view(np.uint8)
    else:
        c = by_word.astype(ml_dtypes.float4_e2m1fn).view(np.uint8) & 0xF
        words = (c[..., 0::2] | (c[..., 1::2] << 4)).reshape(k // 512, 128, 2 * n)
    return np.ascontiguousarray(words), np.ascontiguousarray(byte.astype(np.uint8).reshape(k // 512, 16, n))


def unpack_weight(words, scales, fmt):
    g, _, n = scales.shape
    words = np.ascontiguousarray(words).reshape(g, 128, n, -1)
    if fmt == "e4m3":
        vals = words.view(ml_dtypes.float8_e4m3fn).astype(np.float64)
    else:
        nib = np.empty((g, 128, n, 4), np.uint8)
        nib[..., 0::2] = words & 0xF
        nib[..., 1::2] = words >> 4
        vals = E2M1[nib]
    vals = vals * np.repeat(np.exp2(scales.astype(np.float64) - 127.0), 8, axis=1)[..., None]
    return vals.transpose(0, 1, 3, 2).reshape(g * 512, n)


def sigmoid(v):
    return 1.0 / (1.0 + np.exp(-np.maximum(v, -700.0)))


K, T, E, C, H, HS, N = 512, 768, 6, 256, 512, 512, 256


def by_expert(wq, xq):
    return np.concatenate([wq[e].T @ xq[:, e * C:(e + 1) * C] for e in range(E)], axis=1)


def setup_inputs():
    n = np.random.standard_normal
    s = mx_kscale(K)
    u = mx_kscale(H)
    v = mx_kscale(HS)
    first = np.random.permutation(np.repeat(np.arange(E), T // E))
    second = (first + 1 + np.random.permutation(np.repeat(np.arange(E - 1), -(-T // (E - 1)))[:T])) % E
    while np.bincount(second, minlength=E).max() != T // E:
        load = np.bincount(second, minlength=E); hi, lo = int(load.argmax()), int(load.argmin())
        t = np.flatnonzero((second == hi) & (first != lo))[0]; second[t] = lo
    slot_token = np.empty(E * C, np.int64); pos = np.empty((2, T), np.int64); fill = np.zeros(E, np.int64)
    place = np.stack([np.random.permutation(C) for _ in range(E)])
    for r, deal in enumerate((first, second)):
        for t in np.random.permutation(T):
            e = deal[t]; j = e * C + place[e, fill[e]]; fill[e] += 1; slot_token[j] = t; pos[r, t] = j
    g = np.random.uniform(0.2, 0.8, T)
    x = pack_weight(n((K, T)) * s[:, None], "e4m3")
    w1 = [pack_weight(m, "e2m1") for m in n((E, K, H)) / np.sqrt(K) / s[None, :, None]]
    w3 = [pack_weight(m, "e2m1") for m in n((E, K, H)) / np.sqrt(K) / s[None, :, None] * u]
    w2 = [pack_weight(m, "e2m1") for m in n((E, H, N)) / np.sqrt(H) / u[None, :, None]]
    w1s = pack_weight(n((K, HS)) / np.sqrt(K) / s[:, None], "e4m3")
    w3s = pack_weight(n((K, HS)) / np.sqrt(K) / s[:, None] * v, "e4m3")
    w2s = pack_weight(n((HS, N)) / np.sqrt(HS) / v[:, None], "e4m3")
    return {
        "x_words": x[0],
        "x_scales": x[1],
        "w1_words": np.stack([m[0] for m in w1]),
        "w1_scales": np.stack([m[1] for m in w1]),
        "w3_words": np.stack([m[0] for m in w3]),
        "w3_scales": np.stack([m[1] for m in w3]),
        "w2_words": np.stack([m[0] for m in w2]),
        "w2_scales": np.stack([m[1] for m in w2]),
        "w1s_words": w1s[0],
        "w1s_scales": w1s[1],
        "w3s_words": w3s[0],
        "w3s_scales": w3s[1],
        "w2s_words": w2s[0],
        "w2s_scales": w2s[1],
        "gate": np.stack([np.tile(g, (128, 1)), np.tile(1.0 - g, (128, 1))]).astype(np.float32),
        "offs": striped(slot_token),
        "pos1": striped(pos[0]),
        "pos2": striped(pos[1]),
    }


def reference(x_words, x_scales, w1_words, w1_scales, w3_words, w3_scales, w2_words, w2_scales, w1s_words, w1s_scales, w3s_words, w3s_scales, w2s_words, w2s_scales, gate, offs, pos1, pos2):
    w1 = np.stack([unpack_weight(w1_words[e], w1_scales[e], "e2m1") for e in range(E)])
    w3 = np.stack([unpack_weight(w3_words[e], w3_scales[e], "e2m1") for e in range(E)])
    w2 = np.stack([unpack_weight(w2_words[e], w2_scales[e], "e2m1") for e in range(E)])
    w1s = unpack_weight(w1s_words, w1s_scales, "e4m3")
    w3s = unpack_weight(w3s_words, w3s_scales, "e4m3")
    w2s = unpack_weight(w2s_words, w2s_scales, "e4m3")
    idx = unstriped(offs)
    x = unpack_weight(x_words, x_scales, "e4m3")
    hs = sigmoid(w1s.T @ x) * (w3s.T @ x)
    ys = w2s.T @ mxq(hs, 0, "e4m3")
    h = sigmoid(by_expert(w1, x[:, idx])) * by_expert(w3, x[:, idx])
    y = by_expert(w2, mxq(h, 0, "e4m3"))
    c = sum(f64(gate[r, :1]) * y[:, unstriped(p)] for r, p in enumerate((pos1, pos2)))
    return ys + c

@@ -1,0 +1,186 @@
+from contextlib import ExitStack
+
+import concourse.mybir as mybir
+from concourse.masks import make_identity
+
+K, T, E, C, H, N = 512, 768, 6, 256, 512, 256
+SLOTS = E * C
+FLOPS = 2 * (SLOTS + T) * (2 * K * H + H * N)
+
+F32 = mybir.dt.float32
+BF16 = mybir.dt.bfloat16
+I32 = mybir.dt.int32
+U32 = mybir.dt.uint32
+U16 = mybir.dt.uint16
+U8 = mybir.dt.uint8
+FP8X4 = mybir.dt.float8_e4m3fn_x4
+FP4X4 = mybir.dt.float4_e2m1fn_x4
+MULT = mybir.AluOpType.mult
+ADD = mybir.AluOpType.add
+SIGMOID = mybir.ActivationFunctionType.Sigmoid
+
+P = 128
+GROUP = 256
+LIST_COLS = GROUP // 16
+
+
+def tile_moe_shf_glu_sigmoid_kernel(
+    tc, x_words, x_scales, w1_words, w1_scales, w3_words, w3_scales, w2_words, w2_scales,
+    w1s_words, w1s_scales, w3s_words, w3s_scales, w2s_words, w2s_scales, gate, offs, pos1, pos2, out,
+):
+    nc = tc.nc
+    with ExitStack() as ctx:
+        keep = ctx.enter_context(tc.tile_pool(name="keep", bufs=1))
+        work = ctx.enter_context(tc.tile_pool(name="work", bufs=4))
+        psum = ctx.enter_context(tc.psum_pool(name="psum", bufs=1))
+
+        def held(shape, dtype, name):
+            return keep.tile(shape, dtype, name=name, align_bytes=64)
+
+        offs_sb = keep.tile([P, SLOTS // 16], U16, name="offs_sb")
+        pos1_sb = keep.tile([P, T // 16], U16, name="pos1_sb")
+        pos2_sb = keep.tile([P, T // 16], U16, name="pos2_sb")
+        xw = held([P, T], U32, "xw")
+        xs = held([P, T], U8, "xs")
+        w1w = held([P, E, 2 * H], U8, "w1w")
+        w3w = held([P, E, 2 * H], U8, "w3w")
+        w2w = held([P, E, 2 * N], U8, "w2w")
+        w1p = held([P, E * H], U8, "w1p")
+        w3p = held([P, E * H], U8, "w3p")
+        w2p = held([P, E * N], U8, "w2p")
+        s1w = held([P, H], U32, "s1w")
+        s3w = held([P, H], U32, "s3w")
+        s2w = held([P, N], U32, "s2w")
+        s1p = held([P, H], U8, "s1p")
+        s3p = held([P, H], U8, "s3p")
+        s2p = held([P, N], U8, "s2p")
+        gate_sb = held([P, 2, T], F32, "gate_sb")
+        ident = held([P, P], F32, "ident")
+        warm = held([P, 8], F32, "warm")
+        gw = [held([P, GROUP], U32, "gw%d" % e) for e in range(E)]
+        gs = [held([P, GROUP], U8, "gs%d" % e) for e in range(E)]
+        y = [held([P, SLOTS], F32, "y%d" % n) for n in range(2)]
+        ys = [held([P, T], F32, "ys%d" % n) for n in range(2)]
+
+        def zero(engine, plane):
+            engine.memset(plane.bitcast(I32), 0)
+
+        def load_plane(plane, scales):
+            rows = scales.rearrange("m (q r) c -> r q m c", r=4)
+            for r in range(4):
+                nc.sync.dma_start(plane[r:P:32, :].bitcast(I32).rearrange("q (m c) -> q m c", m=scales.shape[0]), rows[r].bitcast(I32))
+
+        def load_fp4(queue, tile, words, lo, hi):
+            src = words.rearrange("e s p b -> p (e s) b")
+            queue.dma_start(tile[:, lo:hi, :].bitcast(I32), src[:, lo:hi, :].bitcast(I32))
+
+        def load_fp8(queue, tile, words):
+            queue.dma_start(tile[:].bitcast(I32), words[0].rearrange("p c d -> p (c d)").bitcast(I32))
+
+        zero(nc.vector, xs[:])
+        zero(nc.vector, w1p[:])
+        zero(nc.vector, w3p[:])
+        nc.vector.memset(warm[:], 0.0)
+        nc.scalar.activation(warm[:], warm[:], SIGMOID)
+        zero(nc.gpsimd, w2p[:])
+        zero(nc.gpsimd, s1p[:])
+        zero(nc.gpsimd, s3p[:])
+        zero(nc.gpsimd, s2p[:])
+        make_identity(nc, ident[:])
+
+        nc.sync.dma_start(offs_sb[:], offs)
+        load_fp8(nc.sync, xw, x_words)
+        load_fp4(nc.sync, w1w, w1_words, 0, 1)
+        load_fp4(nc.sync, w3w, w3_words, 0, 1)
+        load_plane(xs, x_scales)
+        load_plane(w1p, w1_scales.rearrange("e s b c -> (e s) b c"))
+        load_plane(w3p, w3_scales.rearrange("e s b c -> (e s) b c"))
+        load_plane(w2p, w2_scales.rearrange("e s b c -> (e s) b c"))
+        load_plane(s1p, w1s_scales)
+        load_plane(s3p, w3s_scales)
+        load_plane(s2p, w2s_scales)
+        nc.sync.dma_start(pos1_sb[:], pos1)
+        nc.sync.dma_start(pos2_sb[:], pos2)
+
+        load_fp4(nc.gpsimd, w1w, w1_words, 1, 3)
+        load_fp4(nc.gpsimd, w3w, w3_words, 1, 3)
+        load_fp4(nc.gpsimd, w2w, w2_words, 0, E)
+        load_fp4(nc.gpsimd, w1w, w1_words, 3, E)
+        load_fp4(nc.gpsimd, w3w, w3_words, 3, E)
+        load_fp8(nc.gpsimd, s1w, w1s_words)
+        load_fp8(nc.gpsimd, s3w, w3s_words)
+        load_fp8(nc.gpsimd, s2w, w2s_words)
+        nc.gpsimd.dma_start(gate_sb[:], gate.rearrange("r p t -> p r t"))
+
+        def gather(e):
+            part = offs_sb[:, e * LIST_COLS : (e + 1) * LIST_COLS]
+            nc.vector.tensor_copy(gw[e][:], xw[:].indirect(part))
+            nc.vector.tensor_copy(gs[e][:], xs[:].indirect(part))
+
+        def expert(words, scales, first, third, second, dest):
+            turned = psum.tile([P, 2, 2, P], F32, name="turned", bufs=2)
+            for half in range(2):
+                cols = slice(half * P, (half + 1) * P)
+                a = psum.tile([P, H], F32, name="a", bufs=2)
+                b = psum.tile([P, H], F32, name="b", bufs=3)
+                for acc, (w, plane) in ((a, first), (b, third)):
+                    nc.tensor.matmul_mx(acc[:], lhsT=words[:, cols].bitcast(FP8X4), lhsT_scale=scales[:, cols],
+                                        rhs=w, rhs_scale=plane, start=True, stop=True)
+                sig = work.tile([P, 2, P, 2], F32, name="sig")
+                nc.scalar.activation(sig[:], a[:].rearrange("s (q u e) -> s u q e", u=2, e=2), SIGMOID)
+                h = work.tile([P, H], BF16, name="h", align_bytes=64)
+                nc.vector.tensor_tensor(h[:].rearrange("s (u q e) -> s u q e", u=2, e=2),
+                                        b[:].rearrange("s (q u e) -> s u q e", u=2, e=2), sig[:], MULT)
+                pairs = h[:].bitcast(F32)
+                for u in range(2):
+                    nc.tensor.transpose(turned[:, half, u, :], pairs[:, u * P : (u + 1) * P], ident[:])
+            grouped = work.tile([P, 2 * GROUP], F32, name="grouped", align_bytes=64)
+            nc.scalar.copy(grouped[:].rearrange("p (h s u) -> p h s u", h=2, u=2),
+                           turned[:].rearrange("p h u s -> p h s u"))
+            hw = work.tile([P, GROUP], U32, name="hw", align_bytes=64)
+            hs = work.tile([P, GROUP], U8, name="hs", align_bytes=64)
+            nc.vector.quantize_mx(out=hw[:].bitcast(FP8X4), scales=hs[:], in_=grouped[:].bitcast(BF16))
+            sums = psum.tile([P, 2, GROUP], F32, name="sums", bufs=1)
+            for n in range(2):
+                w, plane = second[n]
+                nc.tensor.matmul_mx(sums[:, n, :], lhsT=w, lhsT_scale=plane, rhs=hw[:].bitcast(FP8X4),
+                                    rhs_scale=hs[:], start=True, stop=True)
+            for n in range(2):
+                nc.scalar.copy(dest[n], sums[:, n, :])
+
+        gather(0)
+        gather(1)
+        for e in range(E):
+            if e + 2 < E:
+                gather(e + 2)
+            cols = slice(e * GROUP, (e + 1) * GROUP)
+            expert(
+                gw[e], gs[e],
+                (w1w[:, e, :].bitcast(FP4X4), w1p[:, e * H : (e + 1) * H]),
+                (w3w[:, e, :].bitcast(FP4X4), w3p[:, e * H : (e + 1) * H]),
+                [(w2w[:, e, 2 * n * P : 2 * (n + 1) * P].bitcast(FP4X4), w2p[:, e * N + n * P : e * N + (n + 1) * P]) for n in range(2)],
+                [y[n][:, cols] for n in range(2)],
+            )
+        for g in range(T // GROUP):
+            cols = slice(g * GROUP, (g + 1) * GROUP)
+            expert(
+                xw[:, cols], xs[:, cols],
+                (s1w[:].bitcast(FP8X4), s1p[:]),
+                (s3w[:].bitcast(FP8X4), s3p[:]),
+                [(s2w[:, n * P : (n + 1) * P].bitcast(FP8X4), s2p[:, n * P : (n + 1) * P]) for n in range(2)],
+                [ys[n][:, cols] for n in range(2)],
+            )
+
+        pieces = [(0, 0, T), (1, 0, 512), (1, 512, T)]
+        picked = []
+        for i, (n, lo, hi) in enumerate(pieces):
+            t1 = held([P, hi - lo], F32, "t1_%d" % i)
+            t2 = held([P, hi - lo], F32, "t2_%d" % i)
+            nc.vector.tensor_tensor(t1[:], y[n][:].indirect(pos1_sb[:, lo // 16 : hi // 16]), gate_sb[:, 0, lo:hi], MULT)
+            nc.vector.tensor_tensor(t2[:], y[n][:].indirect(pos2_sb[:, lo // 16 : hi // 16]), gate_sb[:, 1, lo:hi], MULT)
+            picked.append((t1, t2))
+            part = held([P, hi - lo], F32, "part_%d" % i)
+            total = held([P, hi - lo], F32, "total_%d" % i)
+            nc.vector.tensor_tensor(part[:], t1[:], ys[n][:, lo:hi], ADD)
+            nc.vector.tensor_tensor(total[:], part[:], t2[:], ADD)
+            nc.sync.dma_start(out[n * P : (n + 1) * P, lo:hi], total[:])

@@ -22,6 +22,9 @@ SIGMOID = mybir.ActivationFunctionType.Sigmoid
 P = 128
 GROUP = 256
 LIST_COLS = GROUP // 16
+EARLY = 2
+LEAD = 3
+ON_VECTOR = ((1, 1), (2, 1), (3, 1), (4, 1),)
 
 
 def tile_moe_shf_glu_sigmoid_kernel(
@@ -57,18 +60,23 @@ def tile_moe_shf_glu_sigmoid_kernel(
         gate_sb = held([P, 2, T], F32, "gate_sb")
         ident = held([P, P], F32, "ident")
         warm = held([P, 8], F32, "warm")
-        gw = [held([P, GROUP], U32, "gw%d" % e) for e in range(E)]
-        gs = [held([P, GROUP], U8, "gs%d" % e) for e in range(E)]
         y = [held([P, SLOTS], F32, "y%d" % n) for n in range(2)]
         ys = [held([P, T], F32, "ys%d" % n) for n in range(2)]
 
         def zero(engine, plane):
             engine.memset(plane.bitcast(I32), 0)
 
-        def load_plane(plane, scales):
+        def plane_loads(plane, scales):
             rows = scales.rearrange("m (q r) c -> r q m c", r=4)
-            for r in range(4):
-                nc.sync.dma_start(plane[r:P:32, :].bitcast(I32).rearrange("q (m c) -> q m c", m=scales.shape[0]), rows[r].bitcast(I32))
+            return [
+                (plane[r:P:32, :].bitcast(I32).rearrange("q (m c) -> q m c", m=scales.shape[0]), rows[r].bitcast(I32))
+                for r in range(4)
+            ]
+
+        def load_planes(*planes):
+            for step in zip(*[plane_loads(plane, scales) for plane, scales in planes]):
+                for dst, src in step:
+                    nc.sync.dma_start(dst, src)
 
         def load_fp4(queue, tile, words, lo, hi):
             src = words.rearrange("e s p b -> p (e s) b")
@@ -80,49 +88,48 @@ def tile_moe_shf_glu_sigmoid_kernel(
         zero(nc.vector, xs[:])
         zero(nc.vector, w1p[:])
         zero(nc.vector, w3p[:])
+        zero(nc.vector, w2p[:])
         nc.vector.memset(warm[:], 0.0)
         nc.scalar.activation(warm[:], warm[:], SIGMOID)
-        zero(nc.gpsimd, w2p[:])
+
+        make_identity(nc, ident[:])
         zero(nc.gpsimd, s1p[:])
         zero(nc.gpsimd, s3p[:])
         zero(nc.gpsimd, s2p[:])
-        make_identity(nc, ident[:])
-
-        nc.sync.dma_start(offs_sb[:], offs)
-        load_fp8(nc.sync, xw, x_words)
-        load_fp4(nc.sync, w1w, w1_words, 0, 1)
-        load_fp4(nc.sync, w3w, w3_words, 0, 1)
-        load_plane(xs, x_scales)
-        load_plane(w1p, w1_scales.rearrange("e s b c -> (e s) b c"))
-        load_plane(w3p, w3_scales.rearrange("e s b c -> (e s) b c"))
-        load_plane(w2p, w2_scales.rearrange("e s b c -> (e s) b c"))
-        load_plane(s1p, w1s_scales)
-        load_plane(s3p, w3s_scales)
-        load_plane(s2p, w2s_scales)
-        nc.sync.dma_start(pos1_sb[:], pos1)
-        nc.sync.dma_start(pos2_sb[:], pos2)
-
-        load_fp4(nc.gpsimd, w1w, w1_words, 1, 3)
-        load_fp4(nc.gpsimd, w3w, w3_words, 1, 3)
         load_fp4(nc.gpsimd, w2w, w2_words, 0, E)
-        load_fp4(nc.gpsimd, w1w, w1_words, 3, E)
-        load_fp4(nc.gpsimd, w3w, w3_words, 3, E)
+        load_fp4(nc.gpsimd, w1w, w1_words, EARLY, E)
+        load_fp4(nc.gpsimd, w3w, w3_words, EARLY, E)
         load_fp8(nc.gpsimd, s1w, w1s_words)
         load_fp8(nc.gpsimd, s3w, w3s_words)
         load_fp8(nc.gpsimd, s2w, w2s_words)
         nc.gpsimd.dma_start(gate_sb[:], gate.rearrange("r p t -> p r t"))
 
+        nc.sync.dma_start(offs_sb[:], offs)
+        load_fp8(nc.sync, xw, x_words)
+        load_planes((xs, x_scales))
+        load_fp4(nc.sync, w1w, w1_words, 0, EARLY)
+        load_fp4(nc.sync, w3w, w3_words, 0, EARLY)
+        load_planes((w1p, w1_scales.rearrange("e s b c -> (e s) b c")), (w3p, w3_scales.rearrange("e s b c -> (e s) b c")))
+        load_planes((w2p, w2_scales.rearrange("e s b c -> (e s) b c")))
+        load_planes((s1p, w1s_scales), (s3p, w3s_scales))
+        load_planes((s2p, w2s_scales))
+        nc.sync.dma_start(pos1_sb[:], pos1)
+        nc.sync.dma_start(pos2_sb[:], pos2)
+
         def gather(e):
             part = offs_sb[:, e * LIST_COLS : (e + 1) * LIST_COLS]
-            nc.vector.tensor_copy(gw[e][:], xw[:].indirect(part))
-            nc.vector.tensor_copy(gs[e][:], xs[:].indirect(part))
+            words = work.tile([P, GROUP], U32, name="gw", bufs=2, align_bytes=64)
+            nc.vector.tensor_copy(words[:], xw[:].indirect(part))
+            scales = work.tile([P, GROUP], U8, name="gs", bufs=6, align_bytes=64)
+            nc.vector.tensor_copy(scales[:], xs[:].indirect(part))
+            return words, scales
 
-        def expert(words, scales, first, third, second, dest):
-            turned = psum.tile([P, 2, 2, P], F32, name="turned", bufs=2)
+        def first_layer(words, scales, first, third):
+            hidden = []
             for half in range(2):
                 cols = slice(half * P, (half + 1) * P)
-                a = psum.tile([P, H], F32, name="a", bufs=2)
-                b = psum.tile([P, H], F32, name="b", bufs=3)
+                a = psum.tile([P, H], F32, name="a", tag="a", bufs=2)
+                b = psum.tile([P, H], F32, name="b", tag="b", bufs=3)
                 for acc, (w, plane) in ((a, first), (b, third)):
                     nc.tensor.matmul_mx(acc[:], lhsT=words[:, cols].bitcast(FP8X4), lhsT_scale=scales[:, cols],
                                         rhs=w, rhs_scale=plane, start=True, stop=True)
@@ -131,7 +138,13 @@ def tile_moe_shf_glu_sigmoid_kernel(
                 h = work.tile([P, H], BF16, name="h", align_bytes=64)
                 nc.vector.tensor_tensor(h[:].rearrange("s (u q e) -> s u q e", u=2, e=2),
                                         b[:].rearrange("s (q u e) -> s u q e", u=2, e=2), sig[:], MULT)
-                pairs = h[:].bitcast(F32)
+                hidden.append(h)
+            return hidden
+
+        def quantise(hidden):
+            turned = psum.tile([P, 2, 2, P], F32, name="turned", bufs=1)
+            for half in range(2):
+                pairs = hidden[half][:].bitcast(F32)
                 for u in range(2):
                     nc.tensor.transpose(turned[:, half, u, :], pairs[:, u * P : (u + 1) * P], ident[:])
             grouped = work.tile([P, 2 * GROUP], F32, name="grouped", align_bytes=64)
@@ -140,47 +153,81 @@ def tile_moe_shf_glu_sigmoid_kernel(
             hw = work.tile([P, GROUP], U32, name="hw", align_bytes=64)
             hs = work.tile([P, GROUP], U8, name="hs", align_bytes=64)
             nc.vector.quantize_mx(out=hw[:].bitcast(FP8X4), scales=hs[:], in_=grouped[:].bitcast(BF16))
-            sums = psum.tile([P, 2, GROUP], F32, name="sums", bufs=1)
+            return hw, hs
+
+        def second_layer(g, hw, hs, second, dest):
+            sums = psum.tile([P, 2, GROUP], F32, name="sums", tag="sums", bufs=2)
             for n in range(2):
                 w, plane = second[n]
                 nc.tensor.matmul_mx(sums[:, n, :], lhsT=w, lhsT_scale=plane, rhs=hw[:].bitcast(FP8X4),
                                     rhs_scale=hs[:], start=True, stop=True)
             for n in range(2):
-                nc.scalar.copy(dest[n], sums[:, n, :])
+                if (g, n) in ON_VECTOR:
+                    nc.vector.tensor_copy(dest[n], sums[:, n, :])
+                else:
+                    nc.scalar.copy(dest[n], sums[:, n, :])
 
-        gather(0)
-        gather(1)
-        for e in range(E):
-            if e + 2 < E:
-                gather(e + 2)
-            cols = slice(e * GROUP, (e + 1) * GROUP)
-            expert(
-                gw[e], gs[e],
-                (w1w[:, e, :].bitcast(FP4X4), w1p[:, e * H : (e + 1) * H]),
-                (w3w[:, e, :].bitcast(FP4X4), w3p[:, e * H : (e + 1) * H]),
-                [(w2w[:, e, 2 * n * P : 2 * (n + 1) * P].bitcast(FP4X4), w2p[:, e * N + n * P : e * N + (n + 1) * P]) for n in range(2)],
-                [y[n][:, cols] for n in range(2)],
-            )
-        for g in range(T // GROUP):
-            cols = slice(g * GROUP, (g + 1) * GROUP)
-            expert(
-                xw[:, cols], xs[:, cols],
-                (s1w[:].bitcast(FP8X4), s1p[:]),
-                (s3w[:].bitcast(FP8X4), s3p[:]),
-                [(s2w[:, n * P : (n + 1) * P].bitcast(FP8X4), s2p[:, n * P : (n + 1) * P]) for n in range(2)],
-                [ys[n][:, cols] for n in range(2)],
-            )
+        def first_operands(g):
+            if g < E:
+                return (tokens[g][0], tokens[g][1],
+                        (w1w[:, g, :].bitcast(FP4X4), w1p[:, g * H : (g + 1) * H]),
+                        (w3w[:, g, :].bitcast(FP4X4), w3p[:, g * H : (g + 1) * H]))
+            cols = slice((g - E) * GROUP, (g - E + 1) * GROUP)
+            return xw[:, cols], xs[:, cols], (s1w[:].bitcast(FP8X4), s1p[:]), (s3w[:].bitcast(FP8X4), s3p[:])
 
-        pieces = [(0, 0, T), (1, 0, 512), (1, 512, T)]
-        picked = []
-        for i, (n, lo, hi) in enumerate(pieces):
-            t1 = held([P, hi - lo], F32, "t1_%d" % i)
-            t2 = held([P, hi - lo], F32, "t2_%d" % i)
+        def second_operands(g):
+            if g < E:
+                cols = slice(g * GROUP, (g + 1) * GROUP)
+                return ([(w2w[:, g, 2 * n * P : 2 * (n + 1) * P].bitcast(FP4X4), w2p[:, g * N + n * P : g * N + (n + 1) * P]) for n in range(2)],
+                        [y[n][:, cols] for n in range(2)])
+            cols = slice((g - E) * GROUP, (g - E + 1) * GROUP)
+            return ([(s2w[:, n * P : (n + 1) * P].bitcast(FP8X4), s2p[:, n * P : (n + 1) * P]) for n in range(2)],
+                    [ys[n][:, cols] for n in range(2)])
+
+        groups = E + T // GROUP
+        tokens = [gather(e) for e in range(LEAD)]
+        codes = []
+        for g in range(groups + 1):
+            if g < groups:
+                hidden = first_layer(*first_operands(g))
+                if g + LEAD < E:
+                    tokens.append(gather(g + LEAD))
+                codes.append(quantise(hidden))
+            if g >= 1:
+                second_layer(g - 1, *codes[g - 1], *second_operands(g - 1))
+
+        def pick(n, lo, hi):
+            t1 = held([P, hi - lo], F32, "t1_%d_%d" % (n, lo))
+            t2 = held([P, hi - lo], F32, "t2_%d_%d" % (n, lo))
             nc.vector.tensor_tensor(t1[:], y[n][:].indirect(pos1_sb[:, lo // 16 : hi // 16]), gate_sb[:, 0, lo:hi], MULT)
             nc.vector.tensor_tensor(t2[:], y[n][:].indirect(pos2_sb[:, lo // 16 : hi // 16]), gate_sb[:, 1, lo:hi], MULT)
-            picked.append((t1, t2))
-            part = held([P, hi - lo], F32, "part_%d" % i)
-            total = held([P, hi - lo], F32, "total_%d" % i)
-            nc.vector.tensor_tensor(part[:], t1[:], ys[n][:, lo:hi], ADD)
-            nc.vector.tensor_tensor(total[:], part[:], t2[:], ADD)
+            return t1, t2
+
+        def add_on_tensor(n, lo, hi, terms):
+            blocks = (hi - lo) // P
+            across = psum.tile([P, H], F32, name="across", tag="a", bufs=2)
+            for j in range(blocks):
+                cols = slice(j * P, (j + 1) * P)
+                for i, term in enumerate(terms):
+                    nc.tensor.matmul(across[:, cols], lhsT=term[:, cols], rhs=ident[:], is_transpose=True,
+                                     start=(i == 0), stop=(i == len(terms) - 1))
+            summed = held([P, hi - lo], F32, "summed_%d_%d" % (n, lo))
+            nc.scalar.copy(summed[:], across[:, : hi - lo])
+            back = psum.tile([P, H], F32, name="back", tag="sums", bufs=2)
+            for j in range(blocks):
+                cols = slice(j * P, (j + 1) * P)
+                nc.tensor.transpose(back[:, cols], summed[:, cols], ident[:])
+            total = held([P, hi - lo], F32, "total_%d_%d" % (n, lo))
+            nc.scalar.copy(total[:], back[:, : hi - lo])
             nc.sync.dma_start(out[n * P : (n + 1) * P, lo:hi], total[:])
+
+        def add_on_vector(n, lo, hi, terms):
+            part = held([P, hi - lo], F32, "part_%d_%d" % (n, lo))
+            total = held([P, hi - lo], F32, "total_%d_%d" % (n, lo))
+            nc.vector.tensor_tensor(part[:], terms[1], terms[0], ADD)
+            nc.vector.tensor_tensor(total[:], part[:], terms[2], ADD)
+            nc.sync.dma_start(out[n * P : (n + 1) * P, lo:hi], total[:])
+
+        for n, lo, hi, add in ((0, 0, 512, add_on_tensor), (1, 0, 256, add_on_tensor), (0, 512, 768, add_on_vector), (1, 256, 768, add_on_vector)):
+            t1, t2 = pick(n, lo, hi)
+            add(n, lo, hi, (ys[n][:, lo:hi], t1[:], t2[:]))

@@ -23,8 +23,9 @@ P = 128
 GROUP = 256
 LIST_COLS = GROUP // 16
 EARLY = 2
+MID = 4
 LEAD = 3
-ON_VECTOR = ((1, 1), (2, 1), (3, 1), (4, 1),)
+ON_VECTOR = ((1, 1), (2, 1), (3, 1), (4, 1), (5, 1),)
 
 
 def tile_moe_shf_glu_sigmoid_kernel(
@@ -45,19 +46,15 @@ def tile_moe_shf_glu_sigmoid_kernel(
         pos2_sb = keep.tile([P, T // 16], U16, name="pos2_sb")
         xw = held([P, T], U32, "xw")
         xs = held([P, T], U8, "xs")
-        w1w = held([P, E, 2 * H], U8, "w1w")
-        w3w = held([P, E, 2 * H], U8, "w3w")
-        w2w = held([P, E, 2 * N], U8, "w2w")
+        w1w_early = held([P, MID, 2 * H], U8, "w1w_early")
+        w3w_early = held([P, MID, 2 * H], U8, "w3w_early")
+        w2w_early = held([P, EARLY, 2 * N], U8, "w2w_early")
         w1p = held([P, E * H], U8, "w1p")
         w3p = held([P, E * H], U8, "w3p")
         w2p = held([P, E * N], U8, "w2p")
-        s1w = held([P, H], U32, "s1w")
-        s3w = held([P, H], U32, "s3w")
-        s2w = held([P, N], U32, "s2w")
         s1p = held([P, H], U8, "s1p")
         s3p = held([P, H], U8, "s3p")
         s2p = held([P, N], U8, "s2p")
-        gate_sb = held([P, 2, T], F32, "gate_sb")
         ident = held([P, P], F32, "ident")
         warm = held([P, 8], F32, "warm")
         y = [held([P, SLOTS], F32, "y%d" % n) for n in range(2)]
@@ -80,10 +77,10 @@ def tile_moe_shf_glu_sigmoid_kernel(
 
         def load_fp4(queue, tile, words, lo, hi):
             src = words.rearrange("e s p b -> p (e s) b")
-            queue.dma_start(tile[:, lo:hi, :].bitcast(I32), src[:, lo:hi, :].bitcast(I32))
+            queue.dma_start(tile.bitcast(I32), src[:, lo:hi, :].bitcast(I32))
 
         def load_fp8(queue, tile, words):
-            queue.dma_start(tile[:].bitcast(I32), words[0].rearrange("p c d -> p (c d)").bitcast(I32))
+            queue.dma_start(tile.bitcast(I32), words[0].rearrange("p c d -> p (c d)").bitcast(I32))
 
         zero(nc.vector, xs[:])
         zero(nc.vector, w1p[:])
@@ -96,21 +93,17 @@ def tile_moe_shf_glu_sigmoid_kernel(
         zero(nc.gpsimd, s1p[:])
         zero(nc.gpsimd, s3p[:])
         zero(nc.gpsimd, s2p[:])
-        load_fp4(nc.gpsimd, w2w, w2_words, 0, E)
-        load_fp4(nc.gpsimd, w1w, w1_words, EARLY, E)
-        load_fp4(nc.gpsimd, w3w, w3_words, EARLY, E)
-        load_fp8(nc.gpsimd, s1w, w1s_words)
-        load_fp8(nc.gpsimd, s3w, w3s_words)
-        load_fp8(nc.gpsimd, s2w, w2s_words)
-        nc.gpsimd.dma_start(gate_sb[:], gate.rearrange("r p t -> p r t"))
 
         nc.sync.dma_start(offs_sb[:], offs)
-        load_fp8(nc.sync, xw, x_words)
+        load_fp8(nc.sync, xw[:], x_words)
         load_planes((xs, x_scales))
-        load_fp4(nc.sync, w1w, w1_words, 0, EARLY)
-        load_fp4(nc.sync, w3w, w3_words, 0, EARLY)
+        load_fp4(nc.sync, w1w_early[:, :EARLY, :], w1_words, 0, EARLY)
+        load_fp4(nc.sync, w3w_early[:, :EARLY, :], w3_words, 0, EARLY)
         load_planes((w1p, w1_scales.rearrange("e s b c -> (e s) b c")), (w3p, w3_scales.rearrange("e s b c -> (e s) b c")))
         load_planes((w2p, w2_scales.rearrange("e s b c -> (e s) b c")))
+        load_fp4(nc.sync, w1w_early[:, EARLY:, :], w1_words, EARLY, MID)
+        load_fp4(nc.sync, w3w_early[:, EARLY:, :], w3_words, EARLY, MID)
+        load_fp4(nc.sync, w2w_early[:], w2_words, 0, EARLY)
         load_planes((s1p, w1s_scales), (s3p, w3s_scales))
         load_planes((s2p, w2s_scales))
         nc.sync.dma_start(pos1_sb[:], pos1)
@@ -118,9 +111,15 @@ def tile_moe_shf_glu_sigmoid_kernel(
 
         def gather(e):
             part = offs_sb[:, e * LIST_COLS : (e + 1) * LIST_COLS]
-            words = work.tile([P, GROUP], U32, name="gw", bufs=2, align_bytes=64)
+            if e == 0:
+                words = keep.tile([P, GROUP], U32, name="gw0", tag="words_then_weights", align_bytes=64)
+            else:
+                words = work.tile([P, GROUP], U32, name="gw", bufs=2, align_bytes=64)
             nc.vector.tensor_copy(words[:], xw[:].indirect(part))
-            scales = work.tile([P, GROUP], U8, name="gs", bufs=6, align_bytes=64)
+            if e == 0:
+                scales = keep.tile([P, GROUP], U8, name="gs0", tag="scales_then_gate", align_bytes=64)
+            else:
+                scales = work.tile([P, GROUP], U8, name="gs", bufs=5, align_bytes=64)
             nc.vector.tensor_copy(scales[:], xs[:].indirect(part))
             return words, scales
 
@@ -135,7 +134,7 @@ def tile_moe_shf_glu_sigmoid_kernel(
                                         rhs=w, rhs_scale=plane, start=True, stop=True)
                 sig = work.tile([P, 2, P, 2], F32, name="sig")
                 nc.scalar.activation(sig[:], a[:].rearrange("s (q u e) -> s u q e", u=2, e=2), SIGMOID)
-                h = work.tile([P, H], BF16, name="h", align_bytes=64)
+                h = work.tile([P, H], BF16, name="h", bufs=6, align_bytes=64)
                 nc.vector.tensor_tensor(h[:].rearrange("s (u q e) -> s u q e", u=2, e=2),
                                         b[:].rearrange("s (q u e) -> s u q e", u=2, e=2), sig[:], MULT)
                 hidden.append(h)
@@ -167,34 +166,64 @@ def tile_moe_shf_glu_sigmoid_kernel(
                 else:
                     nc.scalar.copy(dest[n], sums[:, n, :])
 
+        def load_late():
+            widths = [(E - EARLY) * 2 * N, (E - MID) * 2 * H, (E - MID) * 2 * H, 4 * H, 4 * H, 4 * N]
+            late = keep.tile([P, sum(widths)], U8, name="late", tag="words_then_weights", align_bytes=64)
+            parts = [late[:, sum(widths[:i]) : sum(widths[: i + 1])] for i in range(len(widths))]
+            w2w_late = parts[0].rearrange("p (e b) -> p e b", e=E - EARLY)
+            w1w_late = parts[1].rearrange("p (e b) -> p e b", e=E - MID)
+            w3w_late = parts[2].rearrange("p (e b) -> p e b", e=E - MID)
+            load_fp4(nc.gpsimd, w2w_late, w2_words, EARLY, E)
+            load_fp4(nc.gpsimd, w1w_late, w1_words, MID, E)
+            load_fp4(nc.gpsimd, w3w_late, w3_words, MID, E)
+            for part, words in zip(parts[3:], (w1s_words, w3s_words, w2s_words)):
+                load_fp8(nc.gpsimd, part, words)
+            gates = keep.tile([P, 2, T], F32, name="gates", tag="scales_then_gate", align_bytes=64)
+            nc.gpsimd.dma_start(gates[:], gate.rearrange("r p t -> p r t"))
+            w1w.extend(w1w_late[:, e, :] for e in range(E - MID))
+            w3w.extend(w3w_late[:, e, :] for e in range(E - MID))
+            w2w.extend(w2w_late[:, e, :] for e in range(E - EARLY))
+            w1w.append(parts[3])
+            w3w.append(parts[4])
+            w2w.append(parts[5])
+            return gates
+
+        w1w = [w1w_early[:, e, :] for e in range(MID)]
+        w3w = [w3w_early[:, e, :] for e in range(MID)]
+        w2w = [w2w_early[:, e, :] for e in range(EARLY)]
+
         def first_operands(g):
             if g < E:
                 return (tokens[g][0], tokens[g][1],
-                        (w1w[:, g, :].bitcast(FP4X4), w1p[:, g * H : (g + 1) * H]),
-                        (w3w[:, g, :].bitcast(FP4X4), w3p[:, g * H : (g + 1) * H]))
+                        (w1w[g].bitcast(FP4X4), w1p[:, g * H : (g + 1) * H]),
+                        (w3w[g].bitcast(FP4X4), w3p[:, g * H : (g + 1) * H]))
             cols = slice((g - E) * GROUP, (g - E + 1) * GROUP)
-            return xw[:, cols], xs[:, cols], (s1w[:].bitcast(FP8X4), s1p[:]), (s3w[:].bitcast(FP8X4), s3p[:])
+            return xw[:, cols], xs[:, cols], (w1w[E].bitcast(FP8X4), s1p[:]), (w3w[E].bitcast(FP8X4), s3p[:])
 
         def second_operands(g):
             if g < E:
                 cols = slice(g * GROUP, (g + 1) * GROUP)
-                return ([(w2w[:, g, 2 * n * P : 2 * (n + 1) * P].bitcast(FP4X4), w2p[:, g * N + n * P : g * N + (n + 1) * P]) for n in range(2)],
+                return ([(w2w[g][:, 2 * n * P : 2 * (n + 1) * P].bitcast(FP4X4), w2p[:, g * N + n * P : g * N + (n + 1) * P]) for n in range(2)],
                         [y[n][:, cols] for n in range(2)])
             cols = slice((g - E) * GROUP, (g - E + 1) * GROUP)
-            return ([(s2w[:, n * P : (n + 1) * P].bitcast(FP8X4), s2p[:, n * P : (n + 1) * P]) for n in range(2)],
+            return ([(w2w[E][:, 4 * n * P : 4 * (n + 1) * P].bitcast(FP8X4), s2p[:, n * P : (n + 1) * P]) for n in range(2)],
                     [ys[n][:, cols] for n in range(2)])
 
         groups = E + T // GROUP
         tokens = [gather(e) for e in range(LEAD)]
+        hidden = []
         codes = []
-        for g in range(groups + 1):
-            if g < groups:
-                hidden = first_layer(*first_operands(g))
-                if g + LEAD < E:
-                    tokens.append(gather(g + LEAD))
-                codes.append(quantise(hidden))
-            if g >= 1:
-                second_layer(g - 1, *codes[g - 1], *second_operands(g - 1))
+        for step in range(groups + 2):
+            if step < groups:
+                hidden.append(first_layer(*first_operands(step)))
+                if step == 0:
+                    gate_sb = load_late()
+                if step + LEAD < E:
+                    tokens.append(gather(step + LEAD))
+            if 1 <= step <= groups:
+                codes.append(quantise(hidden[step - 1]))
+            if step >= 2:
+                second_layer(step - 2, *codes[step - 2], *second_operands(step - 2))
 
         def pick(n, lo, hi):
             t1 = held([P, hi - lo], F32, "t1_%d_%d" % (n, lo))
@@ -213,7 +242,7 @@ def tile_moe_shf_glu_sigmoid_kernel(
                                      start=(i == 0), stop=(i == len(terms) - 1))
             summed = held([P, hi - lo], F32, "summed_%d_%d" % (n, lo))
             nc.scalar.copy(summed[:], across[:, : hi - lo])
-            back = psum.tile([P, H], F32, name="back", tag="sums", bufs=2)
+            back = psum.tile([P, H], F32, name="back", tag="b", bufs=3)
             for j in range(blocks):
                 cols = slice(j * P, (j + 1) * P)
                 nc.tensor.transpose(back[:, cols], summed[:, cols], ident[:])
@@ -228,6 +257,6 @@ def tile_moe_shf_glu_sigmoid_kernel(
             nc.vector.tensor_tensor(total[:], part[:], terms[2], ADD)
             nc.sync.dma_start(out[n * P : (n + 1) * P, lo:hi], total[:])
 
-        for n, lo, hi, add in ((0, 0, 512, add_on_tensor), (1, 0, 256, add_on_tensor), (0, 512, 768, add_on_vector), (1, 256, 768, add_on_vector)):
+        for n, lo, hi, add in ((0, 0, 256, add_on_tensor), (1, 0, 256, add_on_tensor), (0, 256, 512, add_on_tensor), (1, 256, 512, add_on_tensor), (0, 512, 768, add_on_vector), (1, 512, 768, add_on_vector)):
             t1, t2 = pick(n, lo, hi)
             add(n, lo, hi, (ys[n][:, lo:hi], t1[:], t2[:]))

@@ -48,7 +48,6 @@ def tile_moe_shf_glu_sigmoid_kernel(
         xs = held([P, T], U8, "xs")
         w1w_early = held([P, MID, 2 * H], U8, "w1w_early")
         w3w_early = held([P, MID, 2 * H], U8, "w3w_early")
-        w2w_early = held([P, EARLY, 2 * N], U8, "w2w_early")
         w1p = held([P, E * H], U8, "w1p")
         w3p = held([P, E * H], U8, "w3p")
         w2p = held([P, E * N], U8, "w2p")
@@ -100,14 +99,15 @@ def tile_moe_shf_glu_sigmoid_kernel(
         load_fp4(nc.sync, w1w_early[:, :EARLY, :], w1_words, 0, EARLY)
         load_fp4(nc.sync, w3w_early[:, :EARLY, :], w3_words, 0, EARLY)
         load_planes((w1p, w1_scales.rearrange("e s b c -> (e s) b c")), (w3p, w3_scales.rearrange("e s b c -> (e s) b c")))
-        load_planes((w2p, w2_scales.rearrange("e s b c -> (e s) b c")))
         load_fp4(nc.sync, w1w_early[:, EARLY:, :], w1_words, EARLY, MID)
         load_fp4(nc.sync, w3w_early[:, EARLY:, :], w3_words, EARLY, MID)
-        load_fp4(nc.sync, w2w_early[:], w2_words, 0, EARLY)
+        load_planes((w2p, w2_scales.rearrange("e s b c -> (e s) b c")))
         load_planes((s1p, w1s_scales), (s3p, w3s_scales))
         load_planes((s2p, w2s_scales))
         nc.sync.dma_start(pos1_sb[:], pos1)
         nc.sync.dma_start(pos2_sb[:], pos2)
+
+        pair_scales = []
 
         def gather(e):
             part = offs_sb[:, e * LIST_COLS : (e + 1) * LIST_COLS]
@@ -116,12 +116,14 @@ def tile_moe_shf_glu_sigmoid_kernel(
             else:
                 words = work.tile([P, GROUP], U32, name="gw", bufs=2, align_bytes=64)
             nc.vector.tensor_copy(words[:], xw[:].indirect(part))
-            if e == 0:
-                scales = keep.tile([P, GROUP], U8, name="gs0", tag="scales_then_gate", align_bytes=64)
-            else:
-                scales = work.tile([P, GROUP], U8, name="gs", bufs=5, align_bytes=64)
-            nc.vector.tensor_copy(scales[:], xs[:].indirect(part))
-            return words, scales
+            if e % 2 == 0:
+                if e == 0:
+                    pair = keep.tile([P, 2 * GROUP], U8, name="gs0", tag="scales_then_gate", align_bytes=64)
+                else:
+                    pair = work.tile([P, 2 * GROUP], U8, name="gs", bufs=2, align_bytes=64)
+                nc.vector.tensor_copy(pair[:], xs[:].indirect(offs_sb[:, e * LIST_COLS : (e + 2) * LIST_COLS]))
+                pair_scales.append(pair)
+            return words, pair_scales[e // 2][:, (e % 2) * GROUP : (e % 2 + 1) * GROUP]
 
         def first_layer(words, scales, first, third):
             hidden = []
@@ -141,7 +143,7 @@ def tile_moe_shf_glu_sigmoid_kernel(
             return hidden
 
         def quantise(hidden):
-            turned = psum.tile([P, 2, 2, P], F32, name="turned", bufs=1)
+            turned = psum.tile([P, 2, 2, P], F32, name="turned", tag="turned", bufs=1)
             for half in range(2):
                 pairs = hidden[half][:].bitcast(F32)
                 for u in range(2):
@@ -167,30 +169,27 @@ def tile_moe_shf_glu_sigmoid_kernel(
                     nc.scalar.copy(dest[n], sums[:, n, :])
 
         def load_late():
-            widths = [(E - EARLY) * 2 * N, (E - MID) * 2 * H, (E - MID) * 2 * H, 4 * H, 4 * H, 4 * N]
+            widths = [E * 2 * N, (E - MID) * 2 * H, (E - MID) * 2 * H, 4 * H, 4 * H, 4 * N]
             late = keep.tile([P, sum(widths)], U8, name="late", tag="words_then_weights", align_bytes=64)
             parts = [late[:, sum(widths[:i]) : sum(widths[: i + 1])] for i in range(len(widths))]
-            w2w_late = parts[0].rearrange("p (e b) -> p e b", e=E - EARLY)
+            w2w_late = parts[0].rearrange("p (e b) -> p e b", e=E)
             w1w_late = parts[1].rearrange("p (e b) -> p e b", e=E - MID)
             w3w_late = parts[2].rearrange("p (e b) -> p e b", e=E - MID)
-            load_fp4(nc.gpsimd, w2w_late, w2_words, EARLY, E)
+            load_fp4(nc.gpsimd, w2w_late, w2_words, 0, E)
             load_fp4(nc.gpsimd, w1w_late, w1_words, MID, E)
             load_fp4(nc.gpsimd, w3w_late, w3_words, MID, E)
             for part, words in zip(parts[3:], (w1s_words, w3s_words, w2s_words)):
                 load_fp8(nc.gpsimd, part, words)
-            gates = keep.tile([P, 2, T], F32, name="gates", tag="scales_then_gate", align_bytes=64)
-            nc.gpsimd.dma_start(gates[:], gate.rearrange("r p t -> p r t"))
             w1w.extend(w1w_late[:, e, :] for e in range(E - MID))
             w3w.extend(w3w_late[:, e, :] for e in range(E - MID))
-            w2w.extend(w2w_late[:, e, :] for e in range(E - EARLY))
+            w2w.extend(w2w_late[:, e, :] for e in range(E))
             w1w.append(parts[3])
             w3w.append(parts[4])
             w2w.append(parts[5])
-            return gates
 
         w1w = [w1w_early[:, e, :] for e in range(MID)]
         w3w = [w3w_early[:, e, :] for e in range(MID)]
-        w2w = [w2w_early[:, e, :] for e in range(EARLY)]
+        w2w = []
 
         def first_operands(g):
             if g < E:
@@ -209,6 +208,11 @@ def tile_moe_shf_glu_sigmoid_kernel(
             return ([(w2w[E][:, 4 * n * P : 4 * (n + 1) * P].bitcast(FP8X4), s2p[:, n * P : (n + 1) * P]) for n in range(2)],
                     [ys[n][:, cols] for n in range(2)])
 
+        idle = psum.tile([P, H], F32, name="idle", tag="turned", bufs=1)
+        for i in range(6):
+            nc.tensor.matmul_mx(idle[:], lhsT=xw[:, :P].bitcast(FP8X4), lhsT_scale=xs[:, :P],
+                                rhs=xw[:, :H].bitcast(FP8X4), rhs_scale=xs[:, :H], start=True, stop=True)
+
         groups = E + T // GROUP
         tokens = [gather(e) for e in range(LEAD)]
         hidden = []
@@ -217,7 +221,10 @@ def tile_moe_shf_glu_sigmoid_kernel(
             if step < groups:
                 hidden.append(first_layer(*first_operands(step)))
                 if step == 0:
-                    gate_sb = load_late()
+                    load_late()
+                if step == 1:
+                    gate_sb = keep.tile([P, 2, T], F32, name="gate_sb", tag="scales_then_gate", align_bytes=64)
+                    nc.gpsimd.dma_start(gate_sb[:], gate.rearrange("r p t -> p r t"))
                 if step + LEAD < E:
                     tokens.append(gather(step + LEAD))
             if 1 <= step <= groups:

@@ -21,11 +21,11 @@ SIGMOID = mybir.ActivationFunctionType.Sigmoid
 
 P = 128
 GROUP = 256
-LIST_COLS = GROUP // 16
 EARLY = 2
 MID = 4
-LEAD = 3
-ON_VECTOR = ((1, 1), (2, 1), (3, 1), (4, 1), (5, 1),)
+SPLIT = 6
+ON_VECTOR = ((1,1),(2,1),(3,1),(4,1),(5,1))
+PIECES = ()
 
 
 def tile_moe_shf_glu_sigmoid_kernel(
@@ -48,12 +48,15 @@ def tile_moe_shf_glu_sigmoid_kernel(
         xs = held([P, T], U8, "xs")
         w1w_early = held([P, MID, 2 * H], U8, "w1w_early")
         w3w_early = held([P, MID, 2 * H], U8, "w3w_early")
-        w1p = held([P, E * H], U8, "w1p")
-        w3p = held([P, E * H], U8, "w3p")
+        w1p = [held([P, SPLIT * H], U8, "w1p_a"), None]
+        w3p = [held([P, SPLIT * H], U8, "w3p_a"), None]
         w2p = held([P, E * N], U8, "w2p")
         s1p = held([P, H], U8, "s1p")
         s3p = held([P, H], U8, "s3p")
         s2p = held([P, N], U8, "s2p")
+        w1s_sb = held([P, 4 * H], U8, "w1s_sb")
+        w3s_sb = held([P, 4 * H], U8, "w3s_sb")
+        w2s_sb = held([P, 4 * N], U8, "w2s_sb")
         ident = held([P, P], F32, "ident")
         warm = held([P, 8], F32, "warm")
         y = [held([P, SLOTS], F32, "y%d" % n) for n in range(2)]
@@ -69,10 +72,10 @@ def tile_moe_shf_glu_sigmoid_kernel(
                 for r in range(4)
             ]
 
-        def load_planes(*planes):
+        def load_planes(queue, *planes):
             for step in zip(*[plane_loads(plane, scales) for plane, scales in planes]):
                 for dst, src in step:
-                    nc.sync.dma_start(dst, src)
+                    queue.dma_start(dst, src)
 
         def load_fp4(queue, tile, words, lo, hi):
             src = words.rearrange("e s p b -> p (e s) b")
@@ -81,49 +84,47 @@ def tile_moe_shf_glu_sigmoid_kernel(
         def load_fp8(queue, tile, words):
             queue.dma_start(tile.bitcast(I32), words[0].rearrange("p c d -> p (c d)").bitcast(I32))
 
-        zero(nc.vector, xs[:])
-        zero(nc.vector, w1p[:])
-        zero(nc.vector, w3p[:])
-        zero(nc.vector, w2p[:])
+        w1_rows = w1_scales.rearrange("e s b c -> (e s) b c")
+        w3_rows = w3_scales.rearrange("e s b c -> (e s) b c")
+        w2_rows = w2_scales.rearrange("e s b c -> (e s) b c")
+
+        zero(nc.gpsimd, xs[:])
+        zero(nc.vector, w1p[0][:])
+        zero(nc.vector, w3p[0][:])
         nc.vector.memset(warm[:], 0.0)
         nc.scalar.activation(warm[:], warm[:], SIGMOID)
-
+        zero(nc.vector, w2p[:])
+        if SPLIT < E:
+            zero(nc.vector, w1p[1][:])
+            zero(nc.vector, w3p[1][:])
         make_identity(nc, ident[:])
         zero(nc.gpsimd, s1p[:])
         zero(nc.gpsimd, s3p[:])
         zero(nc.gpsimd, s2p[:])
-
         nc.sync.dma_start(offs_sb[:], offs)
         load_fp8(nc.sync, xw[:], x_words)
-        load_planes((xs, x_scales))
+        load_planes(nc.sync, (xs, x_scales))
         load_fp4(nc.sync, w1w_early[:, :EARLY, :], w1_words, 0, EARLY)
         load_fp4(nc.sync, w3w_early[:, :EARLY, :], w3_words, 0, EARLY)
-        load_planes((w1p, w1_scales.rearrange("e s b c -> (e s) b c")), (w3p, w3_scales.rearrange("e s b c -> (e s) b c")))
+        load_planes(nc.sync, (w1p[0], w1_rows[:SPLIT]), (w3p[0], w3_rows[:SPLIT]))
         load_fp4(nc.sync, w1w_early[:, EARLY:, :], w1_words, EARLY, MID)
         load_fp4(nc.sync, w3w_early[:, EARLY:, :], w3_words, EARLY, MID)
-        load_planes((w2p, w2_scales.rearrange("e s b c -> (e s) b c")))
-        load_planes((s1p, w1s_scales), (s3p, w3s_scales))
-        load_planes((s2p, w2s_scales))
+        load_planes(nc.sync, (w2p, w2_rows))
+        load_planes(nc.sync, (s1p, w1s_scales), (s3p, w3s_scales))
+        load_fp8(nc.sync, w1s_sb[:], w1s_words)
+        load_fp8(nc.sync, w3s_sb[:], w3s_words)
         nc.sync.dma_start(pos1_sb[:], pos1)
         nc.sync.dma_start(pos2_sb[:], pos2)
+        load_planes(nc.sync, (s2p, w2s_scales))
+        load_fp8(nc.sync, w2s_sb[:], w2s_words)
 
-        pair_scales = []
+        slot_words = []
+        slot_scales = []
 
-        def gather(e):
-            part = offs_sb[:, e * LIST_COLS : (e + 1) * LIST_COLS]
-            if e == 0:
-                words = keep.tile([P, GROUP], U32, name="gw0", tag="words_then_weights", align_bytes=64)
-            else:
-                words = work.tile([P, GROUP], U32, name="gw", bufs=2, align_bytes=64)
-            nc.vector.tensor_copy(words[:], xw[:].indirect(part))
-            if e % 2 == 0:
-                if e == 0:
-                    pair = keep.tile([P, 2 * GROUP], U8, name="gs0", tag="scales_then_gate", align_bytes=64)
-                else:
-                    pair = work.tile([P, 2 * GROUP], U8, name="gs", bufs=2, align_bytes=64)
-                nc.vector.tensor_copy(pair[:], xs[:].indirect(offs_sb[:, e * LIST_COLS : (e + 2) * LIST_COLS]))
-                pair_scales.append(pair)
-            return words, pair_scales[e // 2][:, (e % 2) * GROUP : (e % 2 + 1) * GROUP]
+        def gather(source, lo, hi, dtype, into, tag):
+            tile = keep.tile([P, (hi - lo) * C], dtype, name="%s_%d" % (tag, lo), tag=tag, align_bytes=64)
+            nc.vector.tensor_copy(tile[:], source[:].indirect(offs_sb[:, lo * C // 16 : hi * C // 16]))
+            into.extend(tile[:, e * C : (e + 1) * C] for e in range(hi - lo))
 
         def first_layer(words, scales, first, third):
             hidden = []
@@ -168,34 +169,16 @@ def tile_moe_shf_glu_sigmoid_kernel(
                 else:
                     nc.scalar.copy(dest[n], sums[:, n, :])
 
-        def load_late():
-            widths = [E * 2 * N, (E - MID) * 2 * H, (E - MID) * 2 * H, 4 * H, 4 * H, 4 * N]
-            late = keep.tile([P, sum(widths)], U8, name="late", tag="words_then_weights", align_bytes=64)
-            parts = [late[:, sum(widths[:i]) : sum(widths[: i + 1])] for i in range(len(widths))]
-            w2w_late = parts[0].rearrange("p (e b) -> p e b", e=E)
-            w1w_late = parts[1].rearrange("p (e b) -> p e b", e=E - MID)
-            w3w_late = parts[2].rearrange("p (e b) -> p e b", e=E - MID)
-            load_fp4(nc.gpsimd, w2w_late, w2_words, 0, E)
-            load_fp4(nc.gpsimd, w1w_late, w1_words, MID, E)
-            load_fp4(nc.gpsimd, w3w_late, w3_words, MID, E)
-            for part, words in zip(parts[3:], (w1s_words, w3s_words, w2s_words)):
-                load_fp8(nc.gpsimd, part, words)
-            w1w.extend(w1w_late[:, e, :] for e in range(E - MID))
-            w3w.extend(w3w_late[:, e, :] for e in range(E - MID))
-            w2w.extend(w2w_late[:, e, :] for e in range(E))
-            w1w.append(parts[3])
-            w3w.append(parts[4])
-            w2w.append(parts[5])
-
         w1w = [w1w_early[:, e, :] for e in range(MID)]
         w3w = [w3w_early[:, e, :] for e in range(MID)]
         w2w = []
 
         def first_operands(g):
             if g < E:
-                return (tokens[g][0], tokens[g][1],
-                        (w1w[g].bitcast(FP4X4), w1p[:, g * H : (g + 1) * H]),
-                        (w3w[g].bitcast(FP4X4), w3p[:, g * H : (g + 1) * H]))
+                part, at = (0, g) if g < SPLIT else (1, g - SPLIT)
+                return (slot_words[g], slot_scales[g],
+                        (w1w[g].bitcast(FP4X4), w1p[part][:, at * H : (at + 1) * H]),
+                        (w3w[g].bitcast(FP4X4), w3p[part][:, at * H : (at + 1) * H]))
             cols = slice((g - E) * GROUP, (g - E + 1) * GROUP)
             return xw[:, cols], xs[:, cols], (w1w[E].bitcast(FP8X4), s1p[:]), (w3w[E].bitcast(FP8X4), s3p[:])
 
@@ -213,35 +196,16 @@ def tile_moe_shf_glu_sigmoid_kernel(
             nc.tensor.matmul_mx(idle[:], lhsT=xw[:, :P].bitcast(FP8X4), lhsT_scale=xs[:, :P],
                                 rhs=xw[:, :H].bitcast(FP8X4), rhs_scale=xs[:, :H], start=True, stop=True)
 
-        groups = E + T // GROUP
-        tokens = [gather(e) for e in range(LEAD)]
-        hidden = []
-        codes = []
-        for step in range(groups + 2):
-            if step < groups:
-                hidden.append(first_layer(*first_operands(step)))
-                if step == 0:
-                    load_late()
-                if step == 1:
-                    gate_sb = keep.tile([P, 2, T], F32, name="gate_sb", tag="scales_then_gate", align_bytes=64)
-                    nc.gpsimd.dma_start(gate_sb[:], gate.rearrange("r p t -> p r t"))
-                if step + LEAD < E:
-                    tokens.append(gather(step + LEAD))
-            if 1 <= step <= groups:
-                codes.append(quantise(hidden[step - 1]))
-            if step >= 2:
-                second_layer(step - 2, *codes[step - 2], *second_operands(step - 2))
-
         def pick(n, lo, hi):
             t1 = held([P, hi - lo], F32, "t1_%d_%d" % (n, lo))
             t2 = held([P, hi - lo], F32, "t2_%d_%d" % (n, lo))
             nc.vector.tensor_tensor(t1[:], y[n][:].indirect(pos1_sb[:, lo // 16 : hi // 16]), gate_sb[:, 0, lo:hi], MULT)
             nc.vector.tensor_tensor(t2[:], y[n][:].indirect(pos2_sb[:, lo // 16 : hi // 16]), gate_sb[:, 1, lo:hi], MULT)
-            return t1, t2
+            return ys[n][:, lo:hi], t1[:], t2[:]
 
-        def add_on_tensor(n, lo, hi, terms):
+        def add_on_tensor(n, lo, hi, terms, tag="a", bufs=2):
             blocks = (hi - lo) // P
-            across = psum.tile([P, H], F32, name="across", tag="a", bufs=2)
+            across = psum.tile([P, H], F32, name="across", tag=tag, bufs=bufs)
             for j in range(blocks):
                 cols = slice(j * P, (j + 1) * P)
                 for i, term in enumerate(terms):
@@ -264,6 +228,66 @@ def tile_moe_shf_glu_sigmoid_kernel(
             nc.vector.tensor_tensor(total[:], part[:], terms[2], ADD)
             nc.sync.dma_start(out[n * P : (n + 1) * P, lo:hi], total[:])
 
-        for n, lo, hi, add in ((0, 0, 256, add_on_tensor), (1, 0, 256, add_on_tensor), (0, 256, 512, add_on_tensor), (1, 256, 512, add_on_tensor), (0, 512, 768, add_on_vector), (1, 512, 768, add_on_vector)):
-            t1, t2 = pick(n, lo, hi)
-            add(n, lo, hi, (ys[n][:, lo:hi], t1[:], t2[:]))
+        gather(xw, 0, 1, U32, slot_words, "gw0")
+        gather(xs, 0, 2, U8, slot_scales, "gs0")
+        gather(xw, 1, 2, U32, slot_words, "A")
+        gather(xw, 2, 3, U32, slot_words, "B")
+        gather(xs, 2, 4, U8, slot_scales, "C")
+        hidden, codes, picked = {}, {}, {}
+        hidden[0] = first_layer(*first_operands(0))
+        late = keep.tile([P, E * 2 * N + (E - MID) * 2 * H + (E - MID) * 2 * H], U8, name="late", tag="gw0", align_bytes=64)
+        w2w_all = late[:, 0 : 0 + E * 2 * N].rearrange("p (e b) -> p e b", e=E)
+        load_fp4(nc.gpsimd, w2w_all, w2_words, 0, E)
+        w1w_late = late[:, 0 + E * 2 * N : 0 + E * 2 * N + (E - MID) * 2 * H].rearrange("p (e b) -> p e b", e=E - MID)
+        load_fp4(nc.gpsimd, w1w_late, w1_words, MID, E)
+        w3w_late = late[:, 0 + E * 2 * N + (E - MID) * 2 * H : 0 + E * 2 * N + (E - MID) * 2 * H + (E - MID) * 2 * H].rearrange("p (e b) -> p e b", e=E - MID)
+        load_fp4(nc.gpsimd, w3w_late, w3_words, MID, E)
+        w1w.extend([w1w_late[:, e, :] for e in range(E - MID)] + [w1s_sb[:]])
+        w3w.extend([w3w_late[:, e, :] for e in range(E - MID)] + [w3s_sb[:]])
+        w2w.extend([w2w_all[:, e, :] for e in range(E)] + [w2s_sb[:]])
+        gather(xs, 4, 6, U8, slot_scales, "D")
+        hidden[1] = first_layer(*first_operands(1))
+        gate_sb = keep.tile([P, 2, T], F32, name="gate_sb", tag="gs0", align_bytes=64)
+        nc.gpsimd.dma_start(gate_sb[:], gate.rearrange("r p t -> p r t"))
+        gather(xw, 3, 4, U32, slot_words, "A")
+        codes[0] = quantise(hidden[0])
+        hidden[2] = first_layer(*first_operands(2))
+        gather(xw, 4, 5, U32, slot_words, "B")
+        codes[1] = quantise(hidden[1])
+        second_layer(0, *codes[0], *second_operands(0))
+        hidden[3] = first_layer(*first_operands(3))
+        gather(xw, 5, 6, U32, slot_words, "A")
+        codes[2] = quantise(hidden[2])
+        second_layer(1, *codes[1], *second_operands(1))
+        hidden[4] = first_layer(*first_operands(4))
+        codes[3] = quantise(hidden[3])
+        second_layer(2, *codes[2], *second_operands(2))
+        hidden[5] = first_layer(*first_operands(5))
+        codes[4] = quantise(hidden[4])
+        second_layer(3, *codes[3], *second_operands(3))
+        hidden[6] = first_layer(*first_operands(6))
+        codes[5] = quantise(hidden[5])
+        second_layer(4, *codes[4], *second_operands(4))
+        hidden[7] = first_layer(*first_operands(7))
+        codes[6] = quantise(hidden[6])
+        second_layer(5, *codes[5], *second_operands(5))
+        hidden[8] = first_layer(*first_operands(8))
+        codes[7] = quantise(hidden[7])
+        second_layer(6, *codes[6], *second_operands(6))
+        codes[8] = quantise(hidden[8])
+        second_layer(7, *codes[7], *second_operands(7))
+        picked[0,0,256] = pick(0,0,256)
+        add_on_tensor(0,0,256, picked[0,0,256])
+        picked[1,0,256] = pick(1,0,256)
+        add_on_tensor(1,0,256, picked[1,0,256])
+        picked[0,256,512] = pick(0,256,512)
+        add_on_tensor(0,256,512, picked[0,256,512])
+        picked[1,256,512] = pick(1,256,512)
+        add_on_tensor(1,256,512, picked[1,256,512])
+        picked[0,512,768] = pick(0,512,768)
+        picked[1,512,768] = pick(1,512,768)
+        last = psum.tile([P, 2, GROUP], F32, name="last", tag="a", bufs=2)
+        for n, (w, plane) in enumerate(second_operands(8)[0]):
+            nc.tensor.matmul_mx(last[:, n, :], lhsT=w, lhsT_scale=plane, rhs=codes[8][0][:].bitcast(FP8X4), rhs_scale=codes[8][1][:], start=True, stop=True)
+        add_on_vector(0,512,768, (last[:, 0, 0:256],) + picked[0,512,768][1:])
+        add_on_vector(1,512,768, (last[:, 1, 0:256],) + picked[1,512,768][1:])

@@ -57,6 +57,7 @@ def tile_moe_shf_glu_sigmoid_kernel(
         w1s_sb = held([P, 4 * H], U8, "w1s_sb")
         w3s_sb = held([P, 4 * H], U8, "w3s_sb")
         w2s_sb = held([P, 4 * N], U8, "w2s_sb")
+        gate_sb = [held([P, 2, GROUP], F32, "gate%d" % c) for c in range(T // GROUP)]
         ident = held([P, P], F32, "ident")
         warm = held([P, 8], F32, "warm")
         y = [held([P, SLOTS], F32, "y%d" % n) for n in range(2)]
@@ -72,8 +73,8 @@ def tile_moe_shf_glu_sigmoid_kernel(
                 for r in range(4)
             ]
 
-        def load_planes(queue, *planes):
-            for step in zip(*[plane_loads(plane, scales) for plane, scales in planes]):
+        def load_planes(queue, *planes, rows=slice(0, 4)):
+            for step in zip(*[plane_loads(plane, scales)[rows] for plane, scales in planes]):
                 for dst, src in step:
                     queue.dma_start(dst, src)
 
@@ -117,6 +118,9 @@ def tile_moe_shf_glu_sigmoid_kernel(
         nc.sync.dma_start(pos2_sb[:], pos2)
         load_planes(nc.sync, (s2p, w2s_scales))
         load_fp8(nc.sync, w2s_sb[:], w2s_words)
+        nc.sync.dma_start(gate_sb[0][:], gate.rearrange("r p t -> p r t")[:, :, 0 * GROUP : 1 * GROUP])
+        nc.sync.dma_start(gate_sb[1][:], gate.rearrange("r p t -> p r t")[:, :, 1 * GROUP : 2 * GROUP])
+        nc.sync.dma_start(gate_sb[2][:], gate.rearrange("r p t -> p r t")[:, :, 2 * GROUP : 3 * GROUP])
 
         slot_words = []
         slot_scales = []
@@ -126,11 +130,11 @@ def tile_moe_shf_glu_sigmoid_kernel(
             nc.vector.tensor_copy(tile[:], source[:].indirect(offs_sb[:, lo * C // 16 : hi * C // 16]))
             into.extend(tile[:, e * C : (e + 1) * C] for e in range(hi - lo))
 
-        def first_layer(words, scales, first, third):
+        def first_layer(words, scales, first, third, tags=(("a", 2), ("a", 2))):
             hidden = []
             for half in range(2):
                 cols = slice(half * P, (half + 1) * P)
-                a = psum.tile([P, H], F32, name="a", tag="a", bufs=2)
+                a = psum.tile([P, H], F32, name="a", tag=tags[half][0], bufs=tags[half][1])
                 b = psum.tile([P, H], F32, name="b", tag="b", bufs=3)
                 for acc, (w, plane) in ((a, first), (b, third)):
                     nc.tensor.matmul_mx(acc[:], lhsT=words[:, cols].bitcast(FP8X4), lhsT_scale=scales[:, cols],
@@ -199,8 +203,8 @@ def tile_moe_shf_glu_sigmoid_kernel(
         def pick(n, lo, hi):
             t1 = held([P, hi - lo], F32, "t1_%d_%d" % (n, lo))
             t2 = held([P, hi - lo], F32, "t2_%d_%d" % (n, lo))
-            nc.vector.tensor_tensor(t1[:], y[n][:].indirect(pos1_sb[:, lo // 16 : hi // 16]), gate_sb[:, 0, lo:hi], MULT)
-            nc.vector.tensor_tensor(t2[:], y[n][:].indirect(pos2_sb[:, lo // 16 : hi // 16]), gate_sb[:, 1, lo:hi], MULT)
+            nc.vector.tensor_tensor(t1[:], y[n][:].indirect(pos1_sb[:, lo // 16 : hi // 16]), gate_sb[lo // GROUP][:, 0, lo % GROUP : (hi - 1) % GROUP + 1], MULT)
+            nc.vector.tensor_tensor(t2[:], y[n][:].indirect(pos2_sb[:, lo // 16 : hi // 16]), gate_sb[lo // GROUP][:, 1, lo % GROUP : (hi - 1) % GROUP + 1], MULT)
             return ys[n][:, lo:hi], t1[:], t2[:]
 
         def add_on_tensor(n, lo, hi, terms, tag="a", bufs=2):
@@ -237,18 +241,16 @@ def tile_moe_shf_glu_sigmoid_kernel(
         hidden[0] = first_layer(*first_operands(0))
         late = keep.tile([P, E * 2 * N + (E - MID) * 2 * H + (E - MID) * 2 * H], U8, name="late", tag="gw0", align_bytes=64)
         w2w_all = late[:, 0 : 0 + E * 2 * N].rearrange("p (e b) -> p e b", e=E)
-        load_fp4(nc.gpsimd, w2w_all, w2_words, 0, E)
+        load_fp4(nc.scalar, w2w_all, w2_words, 0, E)
         w1w_late = late[:, 0 + E * 2 * N : 0 + E * 2 * N + (E - MID) * 2 * H].rearrange("p (e b) -> p e b", e=E - MID)
-        load_fp4(nc.gpsimd, w1w_late, w1_words, MID, E)
+        load_fp4(nc.scalar, w1w_late, w1_words, MID, E)
         w3w_late = late[:, 0 + E * 2 * N + (E - MID) * 2 * H : 0 + E * 2 * N + (E - MID) * 2 * H + (E - MID) * 2 * H].rearrange("p (e b) -> p e b", e=E - MID)
-        load_fp4(nc.gpsimd, w3w_late, w3_words, MID, E)
+        load_fp4(nc.scalar, w3w_late, w3_words, MID, E)
         w1w.extend([w1w_late[:, e, :] for e in range(E - MID)] + [w1s_sb[:]])
         w3w.extend([w3w_late[:, e, :] for e in range(E - MID)] + [w3s_sb[:]])
         w2w.extend([w2w_all[:, e, :] for e in range(E)] + [w2s_sb[:]])
         gather(xs, 4, 6, U8, slot_scales, "D")
         hidden[1] = first_layer(*first_operands(1))
-        gate_sb = keep.tile([P, 2, T], F32, name="gate_sb", tag="gs0", align_bytes=64)
-        nc.gpsimd.dma_start(gate_sb[:], gate.rearrange("r p t -> p r t"))
         gather(xw, 3, 4, U32, slot_words, "A")
         codes[0] = quantise(hidden[0])
         hidden[2] = first_layer(*first_operands(2))

@@ -21,11 +21,13 @@ SIGMOID = mybir.ActivationFunctionType.Sigmoid
 
 P = 128
 GROUP = 256
-EARLY = 2
-MID = 4
-SPLIT = 6
-ON_VECTOR = ((1,1),(2,1),(3,1),(4,1),(5,1))
-PIECES = ()
+TOKEN_GROUPS = T // GROUP
+GROUPS = E + TOKEN_GROUPS
+ROW_TILES = N // P
+PER_COLUMN = 16
+FIRST_LOAD = 2
+SECOND_LOAD = 4
+WARM_PASSES = 6
 
 
 def tile_moe_shf_glu_sigmoid_kernel(
@@ -38,258 +40,251 @@ def tile_moe_shf_glu_sigmoid_kernel(
         work = ctx.enter_context(tc.tile_pool(name="work", bufs=4))
         psum = ctx.enter_context(tc.psum_pool(name="psum", bufs=1))
 
-        def held(shape, dtype, name):
-            return keep.tile(shape, dtype, name=name, align_bytes=64)
+        def held(shape, dtype, name, tag=None):
+            return keep.tile(shape, dtype, name=name, tag=tag or name, align_bytes=64)
 
-        offs_sb = keep.tile([P, SLOTS // 16], U16, name="offs_sb")
-        pos1_sb = keep.tile([P, T // 16], U16, name="pos1_sb")
-        pos2_sb = keep.tile([P, T // 16], U16, name="pos2_sb")
-        xw = held([P, T], U32, "xw")
-        xs = held([P, T], U8, "xs")
-        w1w_early = held([P, MID, 2 * H], U8, "w1w_early")
-        w3w_early = held([P, MID, 2 * H], U8, "w3w_early")
-        w1p = [held([P, SPLIT * H], U8, "w1p_a"), None]
-        w3p = [held([P, SPLIT * H], U8, "w3p_a"), None]
-        w2p = held([P, E * N], U8, "w2p")
-        s1p = held([P, H], U8, "s1p")
-        s3p = held([P, H], U8, "s3p")
-        s2p = held([P, N], U8, "s2p")
+        def w1_bank(shape, name):
+            return psum.tile(shape, F32, name=name, tag="w1_bank", bufs=2)
+
+        def w3_bank(shape, name):
+            return psum.tile(shape, F32, name=name, tag="w3_bank", bufs=3)
+
+        def turn_bank(shape, name):
+            return psum.tile(shape, F32, name=name, tag="turn_bank", bufs=1)
+
+        offs_sb = keep.tile([P, SLOTS // PER_COLUMN], U16, name="offs_sb")
+        pos1_sb = keep.tile([P, T // PER_COLUMN], U16, name="pos1_sb")
+        pos2_sb = keep.tile([P, T // PER_COLUMN], U16, name="pos2_sb")
+        x_sb = held([P, T], U32, "x_sb")
+        x_plane = held([P, T], U8, "x_plane")
+        w1_early = held([P, SECOND_LOAD, 2 * H], U8, "w1_early")
+        w3_early = held([P, SECOND_LOAD, 2 * H], U8, "w3_early")
+        w1_plane = held([P, E * H], U8, "w1_plane")
+        w3_plane = held([P, E * H], U8, "w3_plane")
+        w2_plane = held([P, E * N], U8, "w2_plane")
+        w1s_plane = held([P, H], U8, "w1s_plane")
+        w3s_plane = held([P, H], U8, "w3s_plane")
+        w2s_plane = held([P, N], U8, "w2s_plane")
         w1s_sb = held([P, 4 * H], U8, "w1s_sb")
         w3s_sb = held([P, 4 * H], U8, "w3s_sb")
         w2s_sb = held([P, 4 * N], U8, "w2s_sb")
-        gate_sb = [held([P, 2, GROUP], F32, "gate%d" % c) for c in range(T // GROUP)]
+        gate_sb = [held([P, 2, GROUP], F32, "gate%d" % c) for c in range(TOKEN_GROUPS)]
         ident = held([P, P], F32, "ident")
-        warm = held([P, 8], F32, "warm")
-        y = [held([P, SLOTS], F32, "y%d" % n) for n in range(2)]
-        ys = [held([P, T], F32, "ys%d" % n) for n in range(2)]
+        table_warm = held([P, 8], F32, "table_warm")
+        y = [held([P, SLOTS], F32, "y%d" % n) for n in range(ROW_TILES)]
+        ys = [held([P, T - GROUP], F32, "ys%d" % n) for n in range(ROW_TILES)]
 
         def zero(engine, plane):
-            engine.memset(plane.bitcast(I32), 0)
+            engine.memset(plane[:].bitcast(I32), 0)
 
-        def plane_loads(plane, scales):
-            rows = scales.rearrange("m (q r) c -> r q m c", r=4)
-            return [
-                (plane[r:P:32, :].bitcast(I32).rearrange("q (m c) -> q m c", m=scales.shape[0]), rows[r].bitcast(I32))
-                for r in range(4)
-            ]
+        def load_planes(*planes):
+            for r in range(4):
+                for plane, scales in planes:
+                    rows = scales.rearrange("m (q r) c -> r q m c", r=4)
+                    dst = plane[r:P:32, :].bitcast(I32).rearrange("q (m c) -> q m c", m=scales.shape[0])
+                    nc.sync.dma_start(dst, rows[r].bitcast(I32))
 
-        def load_planes(queue, *planes, rows=slice(0, 4)):
-            for step in zip(*[plane_loads(plane, scales)[rows] for plane, scales in planes]):
-                for dst, src in step:
-                    queue.dma_start(dst, src)
-
-        def load_fp4(queue, tile, words, lo, hi):
+        def load_fp4(queue, dst, words, lo, hi):
             src = words.rearrange("e s p b -> p (e s) b")
-            queue.dma_start(tile.bitcast(I32), src[:, lo:hi, :].bitcast(I32))
+            queue.dma_start(dst.bitcast(I32), src[:, lo:hi, :].bitcast(I32))
 
-        def load_fp8(queue, tile, words):
-            queue.dma_start(tile.bitcast(I32), words[0].rearrange("p c d -> p (c d)").bitcast(I32))
+        def load_fp8(dst, words):
+            nc.sync.dma_start(dst[:].bitcast(I32), words[0].rearrange("p c d -> p (c d)").bitcast(I32))
 
-        w1_rows = w1_scales.rearrange("e s b c -> (e s) b c")
-        w3_rows = w3_scales.rearrange("e s b c -> (e s) b c")
-        w2_rows = w2_scales.rearrange("e s b c -> (e s) b c")
+        def by_matrix(scales):
+            return scales.rearrange("e s b c -> (e s) b c")
 
-        zero(nc.gpsimd, xs[:])
-        zero(nc.vector, w1p[0][:])
-        zero(nc.vector, w3p[0][:])
-        nc.vector.memset(warm[:], 0.0)
-        nc.scalar.activation(warm[:], warm[:], SIGMOID)
-        zero(nc.vector, w2p[:])
-        if SPLIT < E:
-            zero(nc.vector, w1p[1][:])
-            zero(nc.vector, w3p[1][:])
+        zero(nc.gpsimd, x_plane)
+        zero(nc.vector, w1_plane)
+        zero(nc.vector, w3_plane)
+        nc.vector.memset(table_warm[:], 0.0)
+        nc.scalar.activation(table_warm[:], table_warm[:], SIGMOID)
+        zero(nc.vector, w2_plane)
         make_identity(nc, ident[:])
-        zero(nc.gpsimd, s1p[:])
-        zero(nc.gpsimd, s3p[:])
-        zero(nc.gpsimd, s2p[:])
+        zero(nc.gpsimd, w1s_plane)
+        zero(nc.gpsimd, w3s_plane)
+        zero(nc.gpsimd, w2s_plane)
+
         nc.sync.dma_start(offs_sb[:], offs)
-        load_fp8(nc.sync, xw[:], x_words)
-        load_planes(nc.sync, (xs, x_scales))
-        load_fp4(nc.sync, w1w_early[:, :EARLY, :], w1_words, 0, EARLY)
-        load_fp4(nc.sync, w3w_early[:, :EARLY, :], w3_words, 0, EARLY)
-        load_planes(nc.sync, (w1p[0], w1_rows[:SPLIT]), (w3p[0], w3_rows[:SPLIT]))
-        load_fp4(nc.sync, w1w_early[:, EARLY:, :], w1_words, EARLY, MID)
-        load_fp4(nc.sync, w3w_early[:, EARLY:, :], w3_words, EARLY, MID)
-        load_planes(nc.sync, (w2p, w2_rows))
-        load_planes(nc.sync, (s1p, w1s_scales), (s3p, w3s_scales))
-        load_fp8(nc.sync, w1s_sb[:], w1s_words)
-        load_fp8(nc.sync, w3s_sb[:], w3s_words)
+        load_planes((x_plane, x_scales))
+        load_fp8(x_sb, x_words)
+        load_fp4(nc.sync, w1_early[:, :FIRST_LOAD, :], w1_words, 0, FIRST_LOAD)
+        load_fp4(nc.sync, w3_early[:, :FIRST_LOAD, :], w3_words, 0, FIRST_LOAD)
+        load_planes((w1_plane, by_matrix(w1_scales)), (w3_plane, by_matrix(w3_scales)))
+        load_fp4(nc.sync, w1_early[:, FIRST_LOAD:, :], w1_words, FIRST_LOAD, SECOND_LOAD)
+        load_fp4(nc.sync, w3_early[:, FIRST_LOAD:, :], w3_words, FIRST_LOAD, SECOND_LOAD)
+        load_planes((w2_plane, by_matrix(w2_scales)))
+        load_planes((w1s_plane, w1s_scales), (w3s_plane, w3s_scales))
+        load_fp8(w1s_sb, w1s_words)
+        load_fp8(w3s_sb, w3s_words)
         nc.sync.dma_start(pos1_sb[:], pos1)
         nc.sync.dma_start(pos2_sb[:], pos2)
-        load_planes(nc.sync, (s2p, w2s_scales))
-        load_fp8(nc.sync, w2s_sb[:], w2s_words)
-        nc.sync.dma_start(gate_sb[0][:], gate.rearrange("r p t -> p r t")[:, :, 0 * GROUP : 1 * GROUP])
-        nc.sync.dma_start(gate_sb[1][:], gate.rearrange("r p t -> p r t")[:, :, 1 * GROUP : 2 * GROUP])
-        nc.sync.dma_start(gate_sb[2][:], gate.rearrange("r p t -> p r t")[:, :, 2 * GROUP : 3 * GROUP])
+        load_planes((w2s_plane, w2s_scales))
+        load_fp8(w2s_sb, w2s_words)
+        for c in range(TOKEN_GROUPS):
+            nc.sync.dma_start(gate_sb[c][:], gate.rearrange("r p t -> p r t")[:, :, c * GROUP : (c + 1) * GROUP])
+
+        w1_sb = [w1_early[:, e, :] for e in range(SECOND_LOAD)]
+        w3_sb = [w3_early[:, e, :] for e in range(SECOND_LOAD)]
+        w2_sb = []
+
+        def load_late():
+            left = E - SECOND_LOAD
+            w2_bytes, first_bytes = E * 2 * N, left * 2 * H
+            late = held([P, w2_bytes + 2 * first_bytes], U8, "late", tag="after_expert0")
+            w2_late = late[:, :w2_bytes].rearrange("p (e b) -> p e b", e=E)
+            w1_late = late[:, w2_bytes : w2_bytes + first_bytes].rearrange("p (e b) -> p e b", e=left)
+            w3_late = late[:, w2_bytes + first_bytes :].rearrange("p (e b) -> p e b", e=left)
+            load_fp4(nc.scalar, w2_late, w2_words, 0, E)
+            load_fp4(nc.scalar, w1_late, w1_words, SECOND_LOAD, E)
+            load_fp4(nc.scalar, w3_late, w3_words, SECOND_LOAD, E)
+            w2_sb.extend(w2_late[:, e, :] for e in range(E))
+            w1_sb.extend(w1_late[:, e, :] for e in range(left))
+            w3_sb.extend(w3_late[:, e, :] for e in range(left))
 
         slot_words = []
-        slot_scales = []
+        slot_planes = []
 
-        def gather(source, lo, hi, dtype, into, tag):
-            tile = keep.tile([P, (hi - lo) * C], dtype, name="%s_%d" % (tag, lo), tag=tag, align_bytes=64)
-            nc.vector.tensor_copy(tile[:], source[:].indirect(offs_sb[:, lo * C // 16 : hi * C // 16]))
-            into.extend(tile[:, e * C : (e + 1) * C] for e in range(hi - lo))
+        def gather(source, dtype, lo, hi, into, name, tag):
+            gathered = held([P, (hi - lo) * C], dtype, name, tag)
+            entries = offs_sb[:, lo * C // PER_COLUMN : hi * C // PER_COLUMN]
+            nc.vector.tensor_copy(gathered[:], source[:].indirect(entries))
+            into.extend(gathered[:, e * C : (e + 1) * C] for e in range(hi - lo))
 
-        def first_layer(words, scales, first, third, tags=(("a", 2), ("a", 2))):
-            hidden = []
-            for half in range(2):
+        def gather_words(e, tag):
+            gather(x_sb, U32, e, e + 1, slot_words, "words%d" % e, tag)
+
+        def gather_scales(lo, hi, tag):
+            gather(x_plane, U8, lo, hi, slot_planes, "scales%d" % lo, tag)
+
+        def first_layer(g):
+            if g < E:
+                words, plane = slot_words[g], slot_planes[g]
+                hidden_cols = slice(g * H, (g + 1) * H)
+                first = w1_sb[g].bitcast(FP4X4), w1_plane[:, hidden_cols]
+                third = w3_sb[g].bitcast(FP4X4), w3_plane[:, hidden_cols]
+            else:
+                tokens = slice((g - E) * GROUP, (g - E + 1) * GROUP)
+                words, plane = x_sb[:, tokens], x_plane[:, tokens]
+                first = w1s_sb[:].bitcast(FP8X4), w1s_plane[:]
+                third = w3s_sb[:].bitcast(FP8X4), w3s_plane[:]
+            halves = []
+            for half in range(GROUP // P):
                 cols = slice(half * P, (half + 1) * P)
-                a = psum.tile([P, H], F32, name="a", tag=tags[half][0], bufs=tags[half][1])
-                b = psum.tile([P, H], F32, name="b", tag="b", bufs=3)
-                for acc, (w, plane) in ((a, first), (b, third)):
-                    nc.tensor.matmul_mx(acc[:], lhsT=words[:, cols].bitcast(FP8X4), lhsT_scale=scales[:, cols],
-                                        rhs=w, rhs_scale=plane, start=True, stop=True)
+                a = w1_bank([P, H], "a")
+                b = w3_bank([P, H], "b")
+                for acc, (w, w_plane) in ((a, first), (b, third)):
+                    nc.tensor.matmul_mx(acc[:], lhsT=words[:, cols].bitcast(FP8X4), lhsT_scale=plane[:, cols],
+                                        rhs=w, rhs_scale=w_plane, start=True, stop=True)
                 sig = work.tile([P, 2, P, 2], F32, name="sig")
                 nc.scalar.activation(sig[:], a[:].rearrange("s (q u e) -> s u q e", u=2, e=2), SIGMOID)
                 h = work.tile([P, H], BF16, name="h", bufs=6, align_bytes=64)
                 nc.vector.tensor_tensor(h[:].rearrange("s (u q e) -> s u q e", u=2, e=2),
                                         b[:].rearrange("s (q u e) -> s u q e", u=2, e=2), sig[:], MULT)
-                hidden.append(h)
-            return hidden
+                halves.append(h)
+            return halves
 
-        def quantise(hidden):
-            turned = psum.tile([P, 2, 2, P], F32, name="turned", tag="turned", bufs=1)
-            for half in range(2):
-                pairs = hidden[half][:].bitcast(F32)
+        def quantise(halves):
+            turned = turn_bank([P, 2, 2, P], "turned")
+            for half, h in enumerate(halves):
+                pairs = h[:].bitcast(F32)
                 for u in range(2):
                     nc.tensor.transpose(turned[:, half, u, :], pairs[:, u * P : (u + 1) * P], ident[:])
             grouped = work.tile([P, 2 * GROUP], F32, name="grouped", align_bytes=64)
             nc.scalar.copy(grouped[:].rearrange("p (h s u) -> p h s u", h=2, u=2),
                            turned[:].rearrange("p h u s -> p h s u"))
-            hw = work.tile([P, GROUP], U32, name="hw", align_bytes=64)
-            hs = work.tile([P, GROUP], U8, name="hs", align_bytes=64)
-            nc.vector.quantize_mx(out=hw[:].bitcast(FP8X4), scales=hs[:], in_=grouped[:].bitcast(BF16))
-            return hw, hs
+            h_words = work.tile([P, GROUP], U32, name="h_words", align_bytes=64)
+            h_plane = work.tile([P, GROUP], U8, name="h_plane", align_bytes=64)
+            nc.vector.quantize_mx(out=h_words[:].bitcast(FP8X4), scales=h_plane[:], in_=grouped[:].bitcast(BF16))
+            return h_words, h_plane
 
-        def second_layer(g, hw, hs, second, dest):
-            sums = psum.tile([P, 2, GROUP], F32, name="sums", tag="sums", bufs=2)
-            for n in range(2):
-                w, plane = second[n]
-                nc.tensor.matmul_mx(sums[:, n, :], lhsT=w, lhsT_scale=plane, rhs=hw[:].bitcast(FP8X4),
-                                    rhs_scale=hs[:], start=True, stop=True)
-            for n in range(2):
-                if (g, n) in ON_VECTOR:
-                    nc.vector.tensor_copy(dest[n], sums[:, n, :])
+        def second_products(g, sums, h_words, h_plane):
+            for n in range(ROW_TILES):
+                if g < E:
+                    w = w2_sb[g][:, 2 * n * P : 2 * (n + 1) * P].bitcast(FP4X4)
+                    w_plane = w2_plane[:, g * N + n * P : g * N + (n + 1) * P]
                 else:
-                    nc.scalar.copy(dest[n], sums[:, n, :])
+                    w = w2s_sb[:, 4 * n * P : 4 * (n + 1) * P].bitcast(FP8X4)
+                    w_plane = w2s_plane[:, n * P : (n + 1) * P]
+                nc.tensor.matmul_mx(sums[:, n, :], lhsT=w, lhsT_scale=w_plane, rhs=h_words[:].bitcast(FP8X4),
+                                    rhs_scale=h_plane[:], start=True, stop=True)
 
-        w1w = [w1w_early[:, e, :] for e in range(MID)]
-        w3w = [w3w_early[:, e, :] for e in range(MID)]
-        w2w = []
+        def second_layer(g, h_words, h_plane):
+            sums = psum.tile([P, ROW_TILES, GROUP], F32, name="sums", tag="sums", bufs=2)
+            second_products(g, sums, h_words, h_plane)
+            dest, at = (y, g) if g < E else (ys, g - E)
+            for n in range(ROW_TILES):
+                copy = nc.vector.tensor_copy if n == 1 and 1 <= g < E else nc.scalar.copy
+                copy(dest[n][:, at * GROUP : (at + 1) * GROUP], sums[:, n, :])
 
-        def first_operands(g):
-            if g < E:
-                part, at = (0, g) if g < SPLIT else (1, g - SPLIT)
-                return (slot_words[g], slot_scales[g],
-                        (w1w[g].bitcast(FP4X4), w1p[part][:, at * H : (at + 1) * H]),
-                        (w3w[g].bitcast(FP4X4), w3p[part][:, at * H : (at + 1) * H]))
-            cols = slice((g - E) * GROUP, (g - E + 1) * GROUP)
-            return xw[:, cols], xs[:, cols], (w1w[E].bitcast(FP8X4), s1p[:]), (w3w[E].bitcast(FP8X4), s3p[:])
+        def pick(n, c):
+            entries = slice(c * GROUP // PER_COLUMN, (c + 1) * GROUP // PER_COLUMN)
+            gated = []
+            for r, pos_sb in enumerate((pos1_sb, pos2_sb)):
+                term = held([P, GROUP], F32, "gated%d_%d_%d" % (r, n, c))
+                nc.vector.tensor_tensor(term[:], y[n][:].indirect(pos_sb[:, entries]), gate_sb[c][:, r, :], MULT)
+                gated.append(term)
+            return gated
 
-        def second_operands(g):
-            if g < E:
-                cols = slice(g * GROUP, (g + 1) * GROUP)
-                return ([(w2w[g][:, 2 * n * P : 2 * (n + 1) * P].bitcast(FP4X4), w2p[:, g * N + n * P : g * N + (n + 1) * P]) for n in range(2)],
-                        [y[n][:, cols] for n in range(2)])
-            cols = slice((g - E) * GROUP, (g - E + 1) * GROUP)
-            return ([(w2w[E][:, 4 * n * P : 4 * (n + 1) * P].bitcast(FP8X4), s2p[:, n * P : (n + 1) * P]) for n in range(2)],
-                    [ys[n][:, cols] for n in range(2)])
-
-        idle = psum.tile([P, H], F32, name="idle", tag="turned", bufs=1)
-        for i in range(6):
-            nc.tensor.matmul_mx(idle[:], lhsT=xw[:, :P].bitcast(FP8X4), lhsT_scale=xs[:, :P],
-                                rhs=xw[:, :H].bitcast(FP8X4), rhs_scale=xs[:, :H], start=True, stop=True)
-
-        def pick(n, lo, hi):
-            t1 = held([P, hi - lo], F32, "t1_%d_%d" % (n, lo))
-            t2 = held([P, hi - lo], F32, "t2_%d_%d" % (n, lo))
-            nc.vector.tensor_tensor(t1[:], y[n][:].indirect(pos1_sb[:, lo // 16 : hi // 16]), gate_sb[lo // GROUP][:, 0, lo % GROUP : (hi - 1) % GROUP + 1], MULT)
-            nc.vector.tensor_tensor(t2[:], y[n][:].indirect(pos2_sb[:, lo // 16 : hi // 16]), gate_sb[lo // GROUP][:, 1, lo % GROUP : (hi - 1) % GROUP + 1], MULT)
-            return ys[n][:, lo:hi], t1[:], t2[:]
-
-        def add_on_tensor(n, lo, hi, terms, tag="a", bufs=2):
-            blocks = (hi - lo) // P
-            across = psum.tile([P, H], F32, name="across", tag=tag, bufs=bufs)
-            for j in range(blocks):
+        def add_on_tensor(n, c, gated):
+            terms = [ys[n][:, c * GROUP : (c + 1) * GROUP]] + [term[:] for term in gated]
+            across = w1_bank([P, H], "across")
+            for j in range(GROUP // P):
                 cols = slice(j * P, (j + 1) * P)
                 for i, term in enumerate(terms):
                     nc.tensor.matmul(across[:, cols], lhsT=term[:, cols], rhs=ident[:], is_transpose=True,
                                      start=(i == 0), stop=(i == len(terms) - 1))
-            summed = held([P, hi - lo], F32, "summed_%d_%d" % (n, lo))
-            nc.scalar.copy(summed[:], across[:, : hi - lo])
-            back = psum.tile([P, H], F32, name="back", tag="b", bufs=3)
-            for j in range(blocks):
+            summed = held([P, GROUP], F32, "summed_%d_%d" % (n, c))
+            nc.scalar.copy(summed[:], across[:, :GROUP])
+            back = w3_bank([P, H], "back")
+            for j in range(GROUP // P):
                 cols = slice(j * P, (j + 1) * P)
                 nc.tensor.transpose(back[:, cols], summed[:, cols], ident[:])
-            total = held([P, hi - lo], F32, "total_%d_%d" % (n, lo))
-            nc.scalar.copy(total[:], back[:, : hi - lo])
-            nc.sync.dma_start(out[n * P : (n + 1) * P, lo:hi], total[:])
+            total = held([P, GROUP], F32, "total_%d_%d" % (n, c))
+            nc.scalar.copy(total[:], back[:, :GROUP])
+            nc.sync.dma_start(out[n * P : (n + 1) * P, c * GROUP : (c + 1) * GROUP], total[:])
 
-        def add_on_vector(n, lo, hi, terms):
-            part = held([P, hi - lo], F32, "part_%d_%d" % (n, lo))
-            total = held([P, hi - lo], F32, "total_%d_%d" % (n, lo))
-            nc.vector.tensor_tensor(part[:], terms[1], terms[0], ADD)
-            nc.vector.tensor_tensor(total[:], part[:], terms[2], ADD)
-            nc.sync.dma_start(out[n * P : (n + 1) * P, lo:hi], total[:])
+        def add_on_vector(n, c, gated, shared_sums):
+            part = held([P, GROUP], F32, "part_%d" % n)
+            total = held([P, GROUP], F32, "total_%d_%d" % (n, c))
+            nc.vector.tensor_tensor(part[:], gated[0][:], shared_sums, ADD)
+            nc.vector.tensor_tensor(total[:], part[:], gated[1][:], ADD)
+            nc.sync.dma_start(out[n * P : (n + 1) * P, c * GROUP : (c + 1) * GROUP], total[:])
 
-        gather(xw, 0, 1, U32, slot_words, "gw0")
-        gather(xs, 0, 2, U8, slot_scales, "gs0")
-        gather(xw, 1, 2, U32, slot_words, "A")
-        gather(xw, 2, 3, U32, slot_words, "B")
-        gather(xs, 2, 4, U8, slot_scales, "C")
-        hidden, codes, picked = {}, {}, {}
-        hidden[0] = first_layer(*first_operands(0))
-        late = keep.tile([P, E * 2 * N + (E - MID) * 2 * H + (E - MID) * 2 * H], U8, name="late", tag="gw0", align_bytes=64)
-        w2w_all = late[:, 0 : 0 + E * 2 * N].rearrange("p (e b) -> p e b", e=E)
-        load_fp4(nc.scalar, w2w_all, w2_words, 0, E)
-        w1w_late = late[:, 0 + E * 2 * N : 0 + E * 2 * N + (E - MID) * 2 * H].rearrange("p (e b) -> p e b", e=E - MID)
-        load_fp4(nc.scalar, w1w_late, w1_words, MID, E)
-        w3w_late = late[:, 0 + E * 2 * N + (E - MID) * 2 * H : 0 + E * 2 * N + (E - MID) * 2 * H + (E - MID) * 2 * H].rearrange("p (e b) -> p e b", e=E - MID)
-        load_fp4(nc.scalar, w3w_late, w3_words, MID, E)
-        w1w.extend([w1w_late[:, e, :] for e in range(E - MID)] + [w1s_sb[:]])
-        w3w.extend([w3w_late[:, e, :] for e in range(E - MID)] + [w3s_sb[:]])
-        w2w.extend([w2w_all[:, e, :] for e in range(E)] + [w2s_sb[:]])
-        gather(xs, 4, 6, U8, slot_scales, "D")
-        hidden[1] = first_layer(*first_operands(1))
-        gather(xw, 3, 4, U32, slot_words, "A")
-        codes[0] = quantise(hidden[0])
-        hidden[2] = first_layer(*first_operands(2))
-        gather(xw, 4, 5, U32, slot_words, "B")
-        codes[1] = quantise(hidden[1])
-        second_layer(0, *codes[0], *second_operands(0))
-        hidden[3] = first_layer(*first_operands(3))
-        gather(xw, 5, 6, U32, slot_words, "A")
-        codes[2] = quantise(hidden[2])
-        second_layer(1, *codes[1], *second_operands(1))
-        hidden[4] = first_layer(*first_operands(4))
-        codes[3] = quantise(hidden[3])
-        second_layer(2, *codes[2], *second_operands(2))
-        hidden[5] = first_layer(*first_operands(5))
-        codes[4] = quantise(hidden[4])
-        second_layer(3, *codes[3], *second_operands(3))
-        hidden[6] = first_layer(*first_operands(6))
-        codes[5] = quantise(hidden[5])
-        second_layer(4, *codes[4], *second_operands(4))
-        hidden[7] = first_layer(*first_operands(7))
-        codes[6] = quantise(hidden[6])
-        second_layer(5, *codes[5], *second_operands(5))
-        hidden[8] = first_layer(*first_operands(8))
-        codes[7] = quantise(hidden[7])
-        second_layer(6, *codes[6], *second_operands(6))
-        codes[8] = quantise(hidden[8])
-        second_layer(7, *codes[7], *second_operands(7))
-        picked[0,0,256] = pick(0,0,256)
-        add_on_tensor(0,0,256, picked[0,0,256])
-        picked[1,0,256] = pick(1,0,256)
-        add_on_tensor(1,0,256, picked[1,0,256])
-        picked[0,256,512] = pick(0,256,512)
-        add_on_tensor(0,256,512, picked[0,256,512])
-        picked[1,256,512] = pick(1,256,512)
-        add_on_tensor(1,256,512, picked[1,256,512])
-        picked[0,512,768] = pick(0,512,768)
-        picked[1,512,768] = pick(1,512,768)
-        last = psum.tile([P, 2, GROUP], F32, name="last", tag="a", bufs=2)
-        for n, (w, plane) in enumerate(second_operands(8)[0]):
-            nc.tensor.matmul_mx(last[:, n, :], lhsT=w, lhsT_scale=plane, rhs=codes[8][0][:].bitcast(FP8X4), rhs_scale=codes[8][1][:], start=True, stop=True)
-        add_on_vector(0,512,768, (last[:, 0, 0:256],) + picked[0,512,768][1:])
-        add_on_vector(1,512,768, (last[:, 1, 0:256],) + picked[1,512,768][1:])
+        idle = turn_bank([P, H], "idle")
+        for i in range(WARM_PASSES):
+            nc.tensor.matmul_mx(idle[:], lhsT=x_sb[:, :P].bitcast(FP8X4), lhsT_scale=x_plane[:, :P],
+                                rhs=x_sb[:, :H].bitcast(FP8X4), rhs_scale=x_plane[:, :H], start=True, stop=True)
+
+        for e in range(E - 1):
+            if e % 2 == 0 and e + 2 < E:
+                gather_scales(e, e + 2, "scales%d" % e)
+            gather_words(e, "after_expert%d" % e)
+
+        hidden = []
+        codes = []
+        for step in range(GROUPS + 1):
+            if step < GROUPS:
+                hidden.append(first_layer(step))
+            if step == 0:
+                load_late()
+            if step == 1:
+                gather_scales(E - 2, E - 1, "after_expert1")
+            if step == 2:
+                gather_words(E - 1, "after_expert2")
+            if step == 3:
+                gather_scales(E - 1, E, "after_expert3")
+            if step >= 1:
+                codes.append(quantise(hidden[step - 1]))
+            if step >= 2:
+                second_layer(step - 2, *codes[step - 2])
+
+        last = TOKEN_GROUPS - 1
+        for c in range(last):
+            for n in range(ROW_TILES):
+                add_on_tensor(n, c, pick(n, c))
+        gated_last = [pick(n, last) for n in range(ROW_TILES)]
+        last_sums = w1_bank([P, ROW_TILES, GROUP], "last_sums")
+        second_products(GROUPS - 1, last_sums, *codes[GROUPS - 1])
+        for n in range(ROW_TILES):
+            add_on_vector(n, last, gated_last[n], last_sums[:, n, :])

@@ -25,9 +25,12 @@ TOKEN_GROUPS = T // GROUP
 GROUPS = E + TOKEN_GROUPS
 ROW_TILES = N // P
 PER_COLUMN = 16
-FIRST_LOAD = 2
-SECOND_LOAD = 4
-WARM_PASSES = 6
+FIRST_LOAD = 1
+SECOND_LOAD = 3
+GATHERED_AHEAD = 3
+EARLY_SIGMOIDS = 3
+VECTOR_PIECES = 2
+WARM_PASSES = 4
 
 
 def tile_moe_shf_glu_sigmoid_kernel(
@@ -44,7 +47,7 @@ def tile_moe_shf_glu_sigmoid_kernel(
             return keep.tile(shape, dtype, name=name, tag=tag or name, align_bytes=64)
 
         def w1_bank(shape, name):
-            return psum.tile(shape, F32, name=name, tag="w1_bank", bufs=2)
+            return psum.tile(shape, F32, name=name, tag="w1_bank", bufs=3)
 
         def w3_bank(shape, name):
             return psum.tile(shape, F32, name=name, tag="w3_bank", bufs=3)
@@ -52,13 +55,17 @@ def tile_moe_shf_glu_sigmoid_kernel(
         def turn_bank(shape, name):
             return psum.tile(shape, F32, name=name, tag="turn_bank", bufs=1)
 
+        def sum_bank(shape, name):
+            return psum.tile(shape, F32, name=name, tag="sum_bank", bufs=1)
+
         offs_sb = keep.tile([P, SLOTS // PER_COLUMN], U16, name="offs_sb")
         pos1_sb = keep.tile([P, T // PER_COLUMN], U16, name="pos1_sb")
         pos2_sb = keep.tile([P, T // PER_COLUMN], U16, name="pos2_sb")
         x_sb = held([P, T], U32, "x_sb")
         x_plane = held([P, T], U8, "x_plane")
-        w1_early = held([P, SECOND_LOAD, 2 * H], U8, "w1_early")
-        w3_early = held([P, SECOND_LOAD, 2 * H], U8, "w3_early")
+        w1_sb = held([P, E, 2 * H], U8, "w1_sb")
+        w3_sb = held([P, E, 2 * H], U8, "w3_sb")
+        w2_sb = held([P, E, 2 * N], U8, "w2_sb")
         w1_plane = held([P, E * H], U8, "w1_plane")
         w3_plane = held([P, E * H], U8, "w3_plane")
         w2_plane = held([P, E * N], U8, "w2_plane")
@@ -72,21 +79,20 @@ def tile_moe_shf_glu_sigmoid_kernel(
         ident = held([P, P], F32, "ident")
         table_warm = held([P, 8], F32, "table_warm")
         y = [held([P, SLOTS], F32, "y%d" % n) for n in range(ROW_TILES)]
-        ys = [held([P, T - GROUP], F32, "ys%d" % n) for n in range(ROW_TILES)]
+        ys = [held([P, ROW_TILES, GROUP], F32, "ys%d" % c) for c in range(TOKEN_GROUPS)]
 
         def zero(engine, plane):
             engine.memset(plane[:].bitcast(I32), 0)
 
-        def load_planes(*planes):
+        def load_plane(plane, scales, queue=nc.sync):
             for r in range(4):
-                for plane, scales in planes:
-                    rows = scales.rearrange("m (q r) c -> r q m c", r=4)
-                    dst = plane[r:P:32, :].bitcast(I32).rearrange("q (m c) -> q m c", m=scales.shape[0])
-                    nc.sync.dma_start(dst, rows[r].bitcast(I32))
+                rows = scales.rearrange("m (q r) c -> r q m c", r=4)
+                dst = plane[r:P:32, :].bitcast(I32).rearrange("q (m c) -> q m c", m=scales.shape[0])
+                queue.dma_start(dst, rows[r].bitcast(I32))
 
-        def load_fp4(queue, dst, words, lo, hi):
+        def load_fp4(dst, words, lo, hi):
             src = words.rearrange("e s p b -> p (e s) b")
-            queue.dma_start(dst.bitcast(I32), src[:, lo:hi, :].bitcast(I32))
+            nc.sync.dma_start(dst[:, lo:hi, :].bitcast(I32), src[:, lo:hi, :].bitcast(I32))
 
         def load_fp8(dst, words):
             nc.sync.dma_start(dst[:].bitcast(I32), words[0].rearrange("p c d -> p (c d)").bitcast(I32))
@@ -96,51 +102,38 @@ def tile_moe_shf_glu_sigmoid_kernel(
 
         zero(nc.gpsimd, x_plane)
         zero(nc.vector, w1_plane)
-        zero(nc.vector, w3_plane)
+        zero(nc.vector, w1s_plane)
         nc.vector.memset(table_warm[:], 0.0)
         nc.scalar.activation(table_warm[:], table_warm[:], SIGMOID)
-        zero(nc.vector, w2_plane)
+        zero(nc.vector, w3_plane)
         make_identity(nc, ident[:])
-        zero(nc.gpsimd, w1s_plane)
-        zero(nc.gpsimd, w3s_plane)
-        zero(nc.gpsimd, w2s_plane)
+        zero(nc.gpsimd, w2_plane)
+        zero(nc.vector, w3s_plane)
+        zero(nc.vector, w2s_plane)
+        load_plane(w2_plane, by_matrix(w2_scales), nc.gpsimd)
+        load_plane(w3s_plane, w3s_scales, nc.gpsimd)
 
         nc.sync.dma_start(offs_sb[:], offs)
-        load_planes((x_plane, x_scales))
         load_fp8(x_sb, x_words)
-        load_fp4(nc.sync, w1_early[:, :FIRST_LOAD, :], w1_words, 0, FIRST_LOAD)
-        load_fp4(nc.sync, w3_early[:, :FIRST_LOAD, :], w3_words, 0, FIRST_LOAD)
-        load_planes((w1_plane, by_matrix(w1_scales)), (w3_plane, by_matrix(w3_scales)))
-        load_fp4(nc.sync, w1_early[:, FIRST_LOAD:, :], w1_words, FIRST_LOAD, SECOND_LOAD)
-        load_fp4(nc.sync, w3_early[:, FIRST_LOAD:, :], w3_words, FIRST_LOAD, SECOND_LOAD)
-        load_planes((w2_plane, by_matrix(w2_scales)))
-        load_planes((w1s_plane, w1s_scales), (w3s_plane, w3s_scales))
+        load_fp4(w1_sb, w1_words, 0, FIRST_LOAD)
+        load_plane(x_plane, x_scales)
         load_fp8(w1s_sb, w1s_words)
+        load_plane(w1_plane, by_matrix(w1_scales))
+        load_plane(w1s_plane, w1s_scales)
+        load_fp4(w3_sb, w3_words, 0, FIRST_LOAD)
+        load_plane(w3_plane, by_matrix(w3_scales))
+        load_fp4(w1_sb, w1_words, FIRST_LOAD, SECOND_LOAD)
+        load_fp4(w3_sb, w3_words, FIRST_LOAD, SECOND_LOAD)
+        load_fp4(w2_sb, w2_words, 0, E)
+        load_fp4(w1_sb, w1_words, SECOND_LOAD, E)
+        load_fp4(w3_sb, w3_words, SECOND_LOAD, E)
         load_fp8(w3s_sb, w3s_words)
         nc.sync.dma_start(pos1_sb[:], pos1)
         nc.sync.dma_start(pos2_sb[:], pos2)
-        load_planes((w2s_plane, w2s_scales))
+        load_plane(w2s_plane, w2s_scales)
         load_fp8(w2s_sb, w2s_words)
         for c in range(TOKEN_GROUPS):
             nc.sync.dma_start(gate_sb[c][:], gate.rearrange("r p t -> p r t")[:, :, c * GROUP : (c + 1) * GROUP])
-
-        w1_sb = [w1_early[:, e, :] for e in range(SECOND_LOAD)]
-        w3_sb = [w3_early[:, e, :] for e in range(SECOND_LOAD)]
-        w2_sb = []
-
-        def load_late():
-            left = E - SECOND_LOAD
-            w2_bytes, first_bytes = E * 2 * N, left * 2 * H
-            late = held([P, w2_bytes + 2 * first_bytes], U8, "late", tag="after_expert0")
-            w2_late = late[:, :w2_bytes].rearrange("p (e b) -> p e b", e=E)
-            w1_late = late[:, w2_bytes : w2_bytes + first_bytes].rearrange("p (e b) -> p e b", e=left)
-            w3_late = late[:, w2_bytes + first_bytes :].rearrange("p (e b) -> p e b", e=left)
-            load_fp4(nc.scalar, w2_late, w2_words, 0, E)
-            load_fp4(nc.scalar, w1_late, w1_words, SECOND_LOAD, E)
-            load_fp4(nc.scalar, w3_late, w3_words, SECOND_LOAD, E)
-            w2_sb.extend(w2_late[:, e, :] for e in range(E))
-            w1_sb.extend(w1_late[:, e, :] for e in range(left))
-            w3_sb.extend(w3_late[:, e, :] for e in range(left))
 
         slot_words = []
         slot_planes = []
@@ -151,71 +144,88 @@ def tile_moe_shf_glu_sigmoid_kernel(
             nc.vector.tensor_copy(gathered[:], source[:].indirect(entries))
             into.extend(gathered[:, e * C : (e + 1) * C] for e in range(hi - lo))
 
-        def gather_words(e, tag):
+        def gather_words(e, tag=None):
             gather(x_sb, U32, e, e + 1, slot_words, "words%d" % e, tag)
 
-        def gather_scales(lo, hi, tag):
+        def gather_scales(lo, hi, tag=None):
             gather(x_plane, U8, lo, hi, slot_planes, "scales%d" % lo, tag)
 
-        def first_layer(g):
+        def first_product(acc, g, half, routed, shared):
+            cols = slice(half * P, (half + 1) * P)
             if g < E:
                 words, plane = slot_words[g], slot_planes[g]
-                hidden_cols = slice(g * H, (g + 1) * H)
-                first = w1_sb[g].bitcast(FP4X4), w1_plane[:, hidden_cols]
-                third = w3_sb[g].bitcast(FP4X4), w3_plane[:, hidden_cols]
+                w, w_plane = routed[0][:, g, :].bitcast(FP4X4), routed[1][:, g * H : (g + 1) * H]
             else:
                 tokens = slice((g - E) * GROUP, (g - E + 1) * GROUP)
                 words, plane = x_sb[:, tokens], x_plane[:, tokens]
-                first = w1s_sb[:].bitcast(FP8X4), w1s_plane[:]
-                third = w3s_sb[:].bitcast(FP8X4), w3s_plane[:]
-            halves = []
-            for half in range(GROUP // P):
-                cols = slice(half * P, (half + 1) * P)
-                a = w1_bank([P, H], "a")
-                b = w3_bank([P, H], "b")
-                for acc, (w, w_plane) in ((a, first), (b, third)):
-                    nc.tensor.matmul_mx(acc[:], lhsT=words[:, cols].bitcast(FP8X4), lhsT_scale=plane[:, cols],
-                                        rhs=w, rhs_scale=w_plane, start=True, stop=True)
-                sig = work.tile([P, 2, P, 2], F32, name="sig")
-                nc.scalar.activation(sig[:], a[:].rearrange("s (q u e) -> s u q e", u=2, e=2), SIGMOID)
-                h = work.tile([P, H], BF16, name="h", bufs=6, align_bytes=64)
-                nc.vector.tensor_tensor(h[:].rearrange("s (u q e) -> s u q e", u=2, e=2),
-                                        b[:].rearrange("s (q u e) -> s u q e", u=2, e=2), sig[:], MULT)
-                halves.append(h)
-            return halves
+                w, w_plane = shared[0][:].bitcast(FP8X4), shared[1][:]
+            nc.tensor.matmul_mx(acc[:], lhsT=words[:, cols].bitcast(FP8X4), lhsT_scale=plane[:, cols],
+                                rhs=w, rhs_scale=w_plane, start=True, stop=True)
 
-        def quantise(halves):
-            turned = turn_bank([P, 2, 2, P], "turned")
-            for half, h in enumerate(halves):
-                pairs = h[:].bitcast(F32)
+        sigs = {}
+        hidden = {}
+        turned_sb = {}
+        codes = {}
+
+        def sigmoid(g, halves=range(2)):
+            for half in halves:
+                a = w1_bank([P, H], "a%d%d" % (g, half))
+                first_product(a, g, half, (w1_sb, w1_plane), (w1s_sb, w1s_plane))
+                sig = work.tile([P, 2, P, 2], F32, name="sig%d%d" % (g, half), tag="sig" if g < E else "shared_sig", bufs=4 if g < E else 6)
+                nc.scalar.activation(sig[:], a[:].rearrange("s (q u e) -> s u q e", u=2, e=2), SIGMOID)
+                sigs[g, half] = sig
+
+        def product(g, halves=range(2)):
+            for half in halves:
+                b = w3_bank([P, H], "b%d%d" % (g, half))
+                first_product(b, g, half, (w3_sb, w3_plane), (w3s_sb, w3s_plane))
+                if half == 0:
+                    hidden[g] = work.tile([P, 2, H], BF16, name="hh%d" % g, tag="h" if g < E else "shared_h", bufs=3, align_bytes=64)
+                nc.vector.tensor_tensor(hidden[g][:, half, :].rearrange("s (u q e) -> s u q e", u=2, e=2),
+                                        b[:].rearrange("s (q u e) -> s u q e", u=2, e=2), sigs[g, half][:], MULT)
+
+        def turn(g, bank=turn_bank):
+            turned = bank([P, 2, 2, P], "turned%d" % g)
+            for half in range(2):
+                pairs = hidden[g][:, half, :].bitcast(F32)
                 for u in range(2):
                     nc.tensor.transpose(turned[:, half, u, :], pairs[:, u * P : (u + 1) * P], ident[:])
-            grouped = work.tile([P, 2 * GROUP], F32, name="grouped", align_bytes=64)
+            grouped = work.tile([P, 2 * GROUP], F32, name="grouped%d" % g, tag="grouped", align_bytes=64)
             nc.scalar.copy(grouped[:].rearrange("p (h s u) -> p h s u", h=2, u=2),
                            turned[:].rearrange("p h u s -> p h s u"))
-            h_words = work.tile([P, GROUP], U32, name="h_words", align_bytes=64)
-            h_plane = work.tile([P, GROUP], U8, name="h_plane", align_bytes=64)
-            nc.vector.quantize_mx(out=h_words[:].bitcast(FP8X4), scales=h_plane[:], in_=grouped[:].bitcast(BF16))
-            return h_words, h_plane
+            turned_sb[g] = grouped
 
-        def second_products(g, sums, h_words, h_plane):
-            for n in range(ROW_TILES):
-                if g < E:
-                    w = w2_sb[g][:, 2 * n * P : 2 * (n + 1) * P].bitcast(FP4X4)
-                    w_plane = w2_plane[:, g * N + n * P : g * N + (n + 1) * P]
-                else:
-                    w = w2s_sb[:, 4 * n * P : 4 * (n + 1) * P].bitcast(FP8X4)
-                    w_plane = w2s_plane[:, n * P : (n + 1) * P]
-                nc.tensor.matmul_mx(sums[:, n, :], lhsT=w, lhsT_scale=w_plane, rhs=h_words[:].bitcast(FP8X4),
-                                    rhs_scale=h_plane[:], start=True, stop=True)
+        def quantise(g):
+            h_words = work.tile([P, GROUP], U32, name="h_words%d" % g, tag="h_words", bufs=GROUPS, align_bytes=64)
+            h_plane = work.tile([P, GROUP], U8, name="h_plane%d" % g, tag="h_plane", bufs=GROUPS, align_bytes=64)
+            nc.vector.quantize_mx(out=h_words[:].bitcast(FP8X4), scales=h_plane[:], in_=turned_sb[g][:].bitcast(BF16))
+            codes[g] = h_words, h_plane
 
-        def second_layer(g, h_words, h_plane):
-            sums = psum.tile([P, ROW_TILES, GROUP], F32, name="sums", tag="sums", bufs=2)
-            second_products(g, sums, h_words, h_plane)
-            dest, at = (y, g) if g < E else (ys, g - E)
+        def second_product(g, n, acc):
+            h_words, h_plane = codes[g]
+            if g < E:
+                w = w2_sb[:, g, 2 * n * P : 2 * (n + 1) * P].bitcast(FP4X4)
+                w_plane = w2_plane[:, g * N + n * P : g * N + (n + 1) * P]
+            else:
+                w = w2s_sb[:, 4 * n * P : 4 * (n + 1) * P].bitcast(FP8X4)
+                w_plane = w2s_plane[:, n * P : (n + 1) * P]
+            nc.tensor.matmul_mx(acc, lhsT=w, lhsT_scale=w_plane, rhs=h_words[:].bitcast(FP8X4),
+                                rhs_scale=h_plane[:], start=True, stop=True)
+
+        def second_layer(n, groups, bank=sum_bank):
+            sums = bank([P, len(groups) * GROUP], "sums%d_%d" % (n, groups[0]))
+            for j, g in enumerate(groups):
+                second_product(g, n, sums[:, j * GROUP : (j + 1) * GROUP])
+            dest, at = y, groups[0]
+            copy = nc.vector.tensor_copy if n == 0 and groups[0] == E - 1 else nc.scalar.copy
+            copy(dest[n][:, at * GROUP : (at + len(groups)) * GROUP], sums[:])
+
+        def shared_second_layer(c, bank, rows):
+            sums = bank([P, ROW_TILES, GROUP], "shared_sums%d" % c)
             for n in range(ROW_TILES):
-                copy = nc.vector.tensor_copy if n == 1 and 1 <= g < E else nc.scalar.copy
-                copy(dest[n][:, at * GROUP : (at + 1) * GROUP], sums[:, n, :])
+                second_product(E + c, n, sums[:, n, :])
+            nc.scalar.copy(ys[c][:, :rows, :], sums[:, :rows, :])
+            return sums
 
         def pick(n, c):
             entries = slice(c * GROUP // PER_COLUMN, (c + 1) * GROUP // PER_COLUMN)
@@ -227,8 +237,8 @@ def tile_moe_shf_glu_sigmoid_kernel(
             return gated
 
         def add_on_tensor(n, c, gated):
-            terms = [ys[n][:, c * GROUP : (c + 1) * GROUP]] + [term[:] for term in gated]
-            across = w1_bank([P, H], "across")
+            terms = [ys[c][:, n, :]] + [term[:] for term in gated]
+            across = w1_bank([P, H], "across%d%d" % (n, c))
             for j in range(GROUP // P):
                 cols = slice(j * P, (j + 1) * P)
                 for i, term in enumerate(terms):
@@ -236,16 +246,16 @@ def tile_moe_shf_glu_sigmoid_kernel(
                                      start=(i == 0), stop=(i == len(terms) - 1))
             summed = held([P, GROUP], F32, "summed_%d_%d" % (n, c))
             nc.scalar.copy(summed[:], across[:, :GROUP])
-            back = w3_bank([P, H], "back")
+            back = w3_bank([P, H], "back%d%d" % (n, c))
             for j in range(GROUP // P):
                 cols = slice(j * P, (j + 1) * P)
                 nc.tensor.transpose(back[:, cols], summed[:, cols], ident[:])
             total = held([P, GROUP], F32, "total_%d_%d" % (n, c))
             nc.scalar.copy(total[:], back[:, :GROUP])
-            nc.sync.dma_start(out[n * P : (n + 1) * P, c * GROUP : (c + 1) * GROUP], total[:])
+            nc.scalar.dma_start(out[n * P : (n + 1) * P, c * GROUP : (c + 1) * GROUP], total[:])
 
         def add_on_vector(n, c, gated, shared_sums):
-            part = held([P, GROUP], F32, "part_%d" % n)
+            part = held([P, GROUP], F32, "part_%d" % c)
             total = held([P, GROUP], F32, "total_%d_%d" % (n, c))
             nc.vector.tensor_tensor(part[:], gated[0][:], shared_sums, ADD)
             nc.vector.tensor_tensor(total[:], part[:], gated[1][:], ADD)
@@ -255,36 +265,53 @@ def tile_moe_shf_glu_sigmoid_kernel(
         for i in range(WARM_PASSES):
             nc.tensor.matmul_mx(idle[:], lhsT=x_sb[:, :P].bitcast(FP8X4), lhsT_scale=x_plane[:, :P],
                                 rhs=x_sb[:, :H].bitcast(FP8X4), rhs_scale=x_plane[:, :H], start=True, stop=True)
+        gather_words(0, "words0")
+        gather_words(1, "words1")
+        gather_scales(0, 1)
+        gather_scales(1, 2)
+        gather_scales(2, 4)
+        gather_scales(4, 6)
+        gather_words(2, "words2")
 
-        for e in range(E - 1):
-            if e % 2 == 0 and e + 2 < E:
-                gather_scales(e, e + 2, "scales%d" % e)
-            gather_words(e, "after_expert%d" % e)
-
-        hidden = []
-        codes = []
-        for step in range(GROUPS + 1):
-            if step < GROUPS:
-                hidden.append(first_layer(step))
+        halves = [(g, [half]) for g in range(E, GROUPS) for half in range(2)]
+        gathers_end = E - GATHERED_AHEAD
+        for step in range(E + 2):
+            if step <= gathers_end:
+                sigmoid(step)
+            if step < E:
+                product(step)
             if step == 0:
-                load_late()
+                for g, half in halves[:EARLY_SIGMOIDS]:
+                    sigmoid(g, half)
             if step == 1:
-                gather_scales(E - 2, E - 1, "after_expert1")
-            if step == 2:
-                gather_words(E - 1, "after_expert2")
-            if step == 3:
-                gather_scales(E - 1, E, "after_expert3")
-            if step >= 1:
-                codes.append(quantise(hidden[step - 1]))
+                for g, half in halves[EARLY_SIGMOIDS:4]:
+                    sigmoid(g, half)
+            if gathers_end <= step < E - 1:
+                sigmoid(step + 1)
+            if step < gathers_end:
+                gather_words(step + GATHERED_AHEAD, "words%d" % step)
+            if 1 <= step <= E:
+                turn(step - 1)
+                quantise(step - 1)
             if step >= 2:
-                second_layer(step - 2, *codes[step - 2])
+                second_layer(0, [step - 2])
+            if step == E:
+                sigmoid(GROUPS - 1)
+                for g, half in halves[GATHERED_AHEAD:]:
+                    product(g, half)
+            if gathers_end <= step < E:
+                product(*halves[step - gathers_end])
+        for g in range(E, GROUPS):
+            turn(g, turn_bank if g == GROUPS - 1 else w1_bank)
+            quantise(g)
+        shared_sums = []
+        for c in range(TOKEN_GROUPS):
+            shared_sums.append(shared_second_layer(c, turn_bank if c == 1 else sum_bank, 2 if c == 0 else 1))
+            second_layer(1, [2 * c, 2 * c + 1], w3_bank)
 
-        last = TOKEN_GROUPS - 1
-        for c in range(last):
-            for n in range(ROW_TILES):
-                add_on_tensor(n, c, pick(n, c))
-        gated_last = [pick(n, last) for n in range(ROW_TILES)]
-        last_sums = w1_bank([P, ROW_TILES, GROUP], "last_sums")
-        second_products(GROUPS - 1, last_sums, *codes[GROUPS - 1])
-        for n in range(ROW_TILES):
-            add_on_vector(n, last, gated_last[n], last_sums[:, n, :])
+        pieces = [(n, c) for n in range(ROW_TILES) for c in range(TOKEN_GROUPS)]
+        for n, c in pieces[:-VECTOR_PIECES]:
+            add_on_tensor(n, c, pick(n, c))
+        gated_last = [pick(n, c) for n, c in pieces[-VECTOR_PIECES:]]
+        for j, (n, c) in enumerate(pieces[-VECTOR_PIECES:]):
+            add_on_vector(n, c, gated_last[j], shared_sums[c][:, n, :])

@@ -164,7 +164,10 @@ def tile_moe_shf_glu_sigmoid_kernel(
 
         sigs = {}
         hidden = {}
+        linear = {}
+        turned_ps = {}
         turned_sb = {}
+        sums_ps = {}
         codes = {}
 
         def sigmoid(g, halves=range(2)):
@@ -175,14 +178,18 @@ def tile_moe_shf_glu_sigmoid_kernel(
                 nc.scalar.activation(sig[:], a[:].rearrange("s (q u e) -> s u q e", u=2, e=2), SIGMOID)
                 sigs[g, half] = sig
 
-        def product(g, halves=range(2)):
+        def w3_sums(g, halves=range(2)):
             for half in halves:
                 b = w3_bank([P, H], "b%d%d" % (g, half))
                 first_product(b, g, half, (w3_sb, w3_plane), (w3s_sb, w3s_plane))
+                linear[g, half] = b
+
+        def product(g, halves=range(2)):
+            for half in halves:
                 if half == 0:
                     hidden[g] = work.tile([P, 2, H], BF16, name="hh%d" % g, tag="h" if g < E else "shared_h", bufs=3, align_bytes=64)
                 nc.vector.tensor_tensor(hidden[g][:, half, :].rearrange("s (u q e) -> s u q e", u=2, e=2),
-                                        b[:].rearrange("s (q u e) -> s u q e", u=2, e=2), sigs[g, half][:], MULT)
+                                        linear[g, half][:].rearrange("s (q u e) -> s u q e", u=2, e=2), sigs[g, half][:], MULT)
 
         def turn(g, bank=turn_bank):
             turned = bank([P, 2, 2, P], "turned%d" % g)
@@ -190,9 +197,15 @@ def tile_moe_shf_glu_sigmoid_kernel(
                 pairs = hidden[g][:, half, :].bitcast(F32)
                 for u in range(2):
                     nc.tensor.transpose(turned[:, half, u, :], pairs[:, u * P : (u + 1) * P], ident[:])
-            grouped = work.tile([P, 2 * GROUP], F32, name="grouped%d" % g, tag="grouped", align_bytes=64)
+            turned_ps[g] = turned
+
+        def interleave(g):
+            if g < GROUPS - 1:
+                grouped = work.tile([P, 2 * GROUP], F32, name="grouped%d" % g, tag="grouped", align_bytes=64)
+            else:
+                grouped = held([P, 2 * GROUP], F32, "grouped%d" % g, "after_last_quantise")
             nc.scalar.copy(grouped[:].rearrange("p (h s u) -> p h s u", h=2, u=2),
-                           turned[:].rearrange("p h u s -> p h s u"))
+                           turned_ps[g][:].rearrange("p h u s -> p h s u"))
             turned_sb[g] = grouped
 
         def quantise(g):
@@ -216,9 +229,11 @@ def tile_moe_shf_glu_sigmoid_kernel(
             sums = bank([P, len(groups) * GROUP], "sums%d_%d" % (n, groups[0]))
             for j, g in enumerate(groups):
                 second_product(g, n, sums[:, j * GROUP : (j + 1) * GROUP])
-            dest, at = y, groups[0]
-            copy = nc.vector.tensor_copy if n == 0 and groups[0] == E - 1 else nc.scalar.copy
-            copy(dest[n][:, at * GROUP : (at + len(groups)) * GROUP], sums[:])
+            sums_ps[n, groups[0]] = sums
+
+        def keep_sums(n, g):
+            sums = sums_ps[n, g]
+            nc.scalar.copy(y[n][:, g * GROUP : g * GROUP + sums.shape[1]], sums[:])
 
         def shared_second_layer(c, bank, rows):
             sums = bank([P, ROW_TILES, GROUP], "shared_sums%d" % c)
@@ -227,17 +242,15 @@ def tile_moe_shf_glu_sigmoid_kernel(
             nc.scalar.copy(ys[c][:, :rows, :], sums[:, :rows, :])
             return sums
 
-        def pick(n, c):
+        def pick(n, c, terms):
             entries = slice(c * GROUP // PER_COLUMN, (c + 1) * GROUP // PER_COLUMN)
-            gated = []
+            gated = [terms[:, r * GROUP : (r + 1) * GROUP] for r in range(2)]
             for r, pos_sb in enumerate((pos1_sb, pos2_sb)):
-                term = held([P, GROUP], F32, "gated%d_%d_%d" % (r, n, c))
-                nc.vector.tensor_tensor(term[:], y[n][:].indirect(pos_sb[:, entries]), gate_sb[c][:, r, :], MULT)
-                gated.append(term)
+                nc.vector.tensor_tensor(gated[r], y[n][:].indirect(pos_sb[:, entries]), gate_sb[c][:, r, :], MULT)
             return gated
 
-        def add_on_tensor(n, c, gated):
-            terms = [ys[c][:, n, :]] + [term[:] for term in gated]
+        def add_across(n, c, gated):
+            terms = [ys[c][:, n, :]] + gated
             across = w1_bank([P, H], "across%d%d" % (n, c))
             for j in range(GROUP // P):
                 cols = slice(j * P, (j + 1) * P)
@@ -246,6 +259,9 @@ def tile_moe_shf_glu_sigmoid_kernel(
                                      start=(i == 0), stop=(i == len(terms) - 1))
             summed = held([P, GROUP], F32, "summed_%d_%d" % (n, c))
             nc.scalar.copy(summed[:], across[:, :GROUP])
+            return summed
+
+        def turn_back(n, c, summed):
             back = w3_bank([P, H], "back%d%d" % (n, c))
             for j in range(GROUP // P):
                 cols = slice(j * P, (j + 1) * P)
@@ -254,11 +270,14 @@ def tile_moe_shf_glu_sigmoid_kernel(
             nc.scalar.copy(total[:], back[:, :GROUP])
             nc.scalar.dma_start(out[n * P : (n + 1) * P, c * GROUP : (c + 1) * GROUP], total[:])
 
-        def add_on_vector(n, c, gated, shared_sums):
+        def add_shared(c, gated, shared_sums):
             part = held([P, GROUP], F32, "part_%d" % c)
+            nc.vector.tensor_tensor(part[:], gated[0], shared_sums, ADD)
+            return part
+
+        def add_on_vector(n, c, gated, part):
             total = held([P, GROUP], F32, "total_%d_%d" % (n, c))
-            nc.vector.tensor_tensor(part[:], gated[0][:], shared_sums, ADD)
-            nc.vector.tensor_tensor(total[:], part[:], gated[1][:], ADD)
+            nc.vector.tensor_tensor(total[:], part[:], gated[1], ADD)
             nc.sync.dma_start(out[n * P : (n + 1) * P, c * GROUP : (c + 1) * GROUP], total[:])
 
         idle = turn_bank([P, H], "idle")
@@ -275,43 +294,70 @@ def tile_moe_shf_glu_sigmoid_kernel(
 
         halves = [(g, [half]) for g in range(E, GROUPS) for half in range(2)]
         gathers_end = E - GATHERED_AHEAD
-        for step in range(E + 2):
-            if step <= gathers_end:
-                sigmoid(step)
-            if step < E:
-                product(step)
+        sigmoid(0)
+        for g, half in halves[:EARLY_SIGMOIDS]:
+            sigmoid(g, half)
+        w3_sums(0)
+        for step in range(E):
+            if step >= 1:
+                interleave(step - 1)
+            if step >= 2:
+                keep_sums(0, step - 2)
+            sigmoid(step + 1 if step + 1 < E else GROUPS - 1)
             if step == 0:
-                for g, half in halves[:EARLY_SIGMOIDS]:
-                    sigmoid(g, half)
-            if step == 1:
                 for g, half in halves[EARLY_SIGMOIDS:4]:
                     sigmoid(g, half)
-            if gathers_end <= step < E - 1:
-                sigmoid(step + 1)
+            if step >= gathers_end:
+                w3_sums(*halves[step - gathers_end])
+            w3_sums(*((step + 1, range(2)) if step + 1 < E else halves[GATHERED_AHEAD]))
+            product(step)
+            turn(step)
+            if step >= 1:
+                quantise(step - 1)
+                second_layer(0, [step - 1])
             if step < gathers_end:
                 gather_words(step + GATHERED_AHEAD, "words%d" % step)
-            if 1 <= step <= E:
-                turn(step - 1)
-                quantise(step - 1)
-            if step >= 2:
-                second_layer(0, [step - 2])
-            if step == E:
-                sigmoid(GROUPS - 1)
-                for g, half in halves[GATHERED_AHEAD:]:
-                    product(g, half)
-            if gathers_end <= step < E:
+            else:
                 product(*halves[step - gathers_end])
-        for g in range(E, GROUPS):
-            turn(g, turn_bank if g == GROUPS - 1 else w1_bank)
-            quantise(g)
-        shared_sums = []
-        for c in range(TOKEN_GROUPS):
-            shared_sums.append(shared_second_layer(c, turn_bank if c == 1 else sum_bank, 2 if c == 0 else 1))
-            second_layer(1, [2 * c, 2 * c + 1], w3_bank)
+
+        last = E - 1
+        interleave(last)
+        keep_sums(0, last - 1)
+        w3_sums(E + 2)
+        product(E + 1, [1])
+        product(E + 2, [0])
+        turn(E, w1_bank)
+        interleave(E)
+        quantise(last)
+        turn(E + 1, w1_bank)
+        interleave(E + 1)
+        second_layer(0, [last])
+        keep_sums(0, last)
+        product(E + 2, [1])
+        quantise(E)
+        quantise(E + 1)
+        second_layer(1, [0, 1], w3_bank)
+        keep_sums(1, 0)
+        turn(E + 2)
+        interleave(E + 2)
 
         pieces = [(n, c) for n in range(ROW_TILES) for c in range(TOKEN_GROUPS)]
-        for n, c in pieces[:-VECTOR_PIECES]:
-            add_on_tensor(n, c, pick(n, c))
-        gated_last = [pick(n, c) for n, c in pieces[-VECTOR_PIECES:]]
-        for j, (n, c) in enumerate(pieces[-VECTOR_PIECES:]):
-            add_on_vector(n, c, gated_last[j], shared_sums[c][:, n, :])
+        shared_sums = [shared_second_layer(0, sum_bank, 2), shared_second_layer(1, w1_bank, 1)]
+        for e in range(2, E, 2):
+            second_layer(1, [e, e + 1], w3_bank)
+            keep_sums(1, e)
+        gated = [pick(0, 0, held([P, 2 * GROUP], F32, "first_terms"))]
+        quantise(E + 2)
+        shared_sums.append(shared_second_layer(2, turn_bank, 1))
+        later_terms = held([P, 2 * GROUP * (len(pieces) - 1)], F32, "later_terms", "after_last_quantise")
+        for j, (n, c) in enumerate(pieces[1:]):
+            gated.append(pick(n, c, later_terms[:, 2 * j * GROUP : 2 * (j + 1) * GROUP]))
+        on_tensor = len(pieces) - VECTOR_PIECES
+        summed = [add_across(n, c, gated[j]) for j, (n, c) in enumerate(pieces[:1])]
+        for j in range(on_tensor):
+            if j + 1 < on_tensor:
+                summed.append(add_across(*pieces[j + 1], gated[j + 1]))
+            turn_back(*pieces[j], summed[j])
+        parts = [add_shared(c, gated[on_tensor + j], shared_sums[c][:, n, :]) for j, (n, c) in enumerate(pieces[on_tensor:])]
+        for j, (n, c) in enumerate(pieces[on_tensor:]):
+            add_on_vector(n, c, gated[on_tensor + j], parts[j])

@@ -29,8 +29,6 @@ FIRST_LOAD = 1
 SECOND_LOAD = 3
 GATHERED_AHEAD = 3
 EARLY_SIGMOIDS = 3
-VECTOR_PIECES = 2
-WARM_PASSES = 4
 
 
 def tile_moe_shf_glu_sigmoid_kernel(
@@ -63,8 +61,11 @@ def tile_moe_shf_glu_sigmoid_kernel(
         pos2_sb = keep.tile([P, T // PER_COLUMN], U16, name="pos2_sb")
         x_sb = held([P, T], U32, "x_sb")
         x_plane = held([P, T], U8, "x_plane")
-        w1_sb = held([P, E, 2 * H], U8, "w1_sb")
-        w3_sb = held([P, E, 2 * H], U8, "w3_sb")
+        w1_first = held([P, FIRST_LOAD, 2 * H], U8, "w1_first", "until_expert2")
+        w1_rest = held([P, E - FIRST_LOAD, 2 * H], U8, "w1_rest")
+        w1_sb = [w1_first[:, e, :] for e in range(FIRST_LOAD)] + [w1_rest[:, e, :] for e in range(E - FIRST_LOAD)]
+        w3_all = held([P, E, 2 * H], U8, "w3_all")
+        w3_sb = [w3_all[:, e, :] for e in range(E)]
         w2_sb = held([P, E, 2 * N], U8, "w2_sb")
         w1_plane = held([P, E * H], U8, "w1_plane")
         w3_plane = held([P, E * H], U8, "w3_plane")
@@ -92,7 +93,7 @@ def tile_moe_shf_glu_sigmoid_kernel(
 
         def load_fp4(dst, words, lo, hi):
             src = words.rearrange("e s p b -> p (e s) b")
-            nc.sync.dma_start(dst[:, lo:hi, :].bitcast(I32), src[:, lo:hi, :].bitcast(I32))
+            nc.sync.dma_start(dst.bitcast(I32), src[:, lo:hi, :].bitcast(I32))
 
         def load_fp8(dst, words):
             nc.sync.dma_start(dst[:].bitcast(I32), words[0].rearrange("p c d -> p (c d)").bitcast(I32))
@@ -113,20 +114,20 @@ def tile_moe_shf_glu_sigmoid_kernel(
         load_plane(w2_plane, by_matrix(w2_scales), nc.gpsimd)
         load_plane(w3s_plane, w3s_scales, nc.gpsimd)
 
-        nc.sync.dma_start(offs_sb[:], offs)
         load_fp8(x_sb, x_words)
-        load_fp4(w1_sb, w1_words, 0, FIRST_LOAD)
+        nc.sync.dma_start(offs_sb[:], offs)
         load_plane(x_plane, x_scales)
-        load_fp8(w1s_sb, w1s_words)
+        load_fp4(w1_first[:], w1_words, 0, FIRST_LOAD)
         load_plane(w1_plane, by_matrix(w1_scales))
         load_plane(w1s_plane, w1s_scales)
-        load_fp4(w3_sb, w3_words, 0, FIRST_LOAD)
+        load_fp8(w1s_sb, w1s_words)
+        load_fp4(w3_all[:, :FIRST_LOAD, :], w3_words, 0, FIRST_LOAD)
         load_plane(w3_plane, by_matrix(w3_scales))
-        load_fp4(w1_sb, w1_words, FIRST_LOAD, SECOND_LOAD)
-        load_fp4(w3_sb, w3_words, FIRST_LOAD, SECOND_LOAD)
-        load_fp4(w2_sb, w2_words, 0, E)
-        load_fp4(w1_sb, w1_words, SECOND_LOAD, E)
-        load_fp4(w3_sb, w3_words, SECOND_LOAD, E)
+        load_fp4(w1_rest[:, : SECOND_LOAD - FIRST_LOAD, :], w1_words, FIRST_LOAD, SECOND_LOAD)
+        load_fp4(w3_all[:, FIRST_LOAD:SECOND_LOAD, :], w3_words, FIRST_LOAD, SECOND_LOAD)
+        load_fp4(w2_sb[:], w2_words, 0, E)
+        load_fp4(w1_rest[:, SECOND_LOAD - FIRST_LOAD :, :], w1_words, SECOND_LOAD, E)
+        load_fp4(w3_all[:, SECOND_LOAD:, :], w3_words, SECOND_LOAD, E)
         load_fp8(w3s_sb, w3s_words)
         nc.sync.dma_start(pos1_sb[:], pos1)
         nc.sync.dma_start(pos2_sb[:], pos2)
@@ -138,23 +139,22 @@ def tile_moe_shf_glu_sigmoid_kernel(
         slot_words = []
         slot_planes = []
 
-        def gather(source, dtype, lo, hi, into, name, tag):
-            gathered = held([P, (hi - lo) * C], dtype, name, tag)
+        def gather(source, gathered, lo, hi, into):
             entries = offs_sb[:, lo * C // PER_COLUMN : hi * C // PER_COLUMN]
-            nc.vector.tensor_copy(gathered[:], source[:].indirect(entries))
+            nc.vector.tensor_copy(gathered, source[:].indirect(entries))
             into.extend(gathered[:, e * C : (e + 1) * C] for e in range(hi - lo))
 
-        def gather_words(e, tag=None):
-            gather(x_sb, U32, e, e + 1, slot_words, "words%d" % e, tag)
+        def gather_words(e, gathered):
+            gather(x_sb, gathered, e, e + 1, slot_words)
 
         def gather_scales(lo, hi, tag=None):
-            gather(x_plane, U8, lo, hi, slot_planes, "scales%d" % lo, tag)
+            gather(x_plane, held([P, (hi - lo) * C], U8, "scales%d" % lo, tag)[:], lo, hi, slot_planes)
 
         def first_product(acc, g, half, routed, shared):
             cols = slice(half * P, (half + 1) * P)
             if g < E:
                 words, plane = slot_words[g], slot_planes[g]
-                w, w_plane = routed[0][:, g, :].bitcast(FP4X4), routed[1][:, g * H : (g + 1) * H]
+                w, w_plane = routed[0][g].bitcast(FP4X4), routed[1][:, g * H : (g + 1) * H]
             else:
                 tokens = slice((g - E) * GROUP, (g - E + 1) * GROUP)
                 words, plane = x_sb[:, tokens], x_plane[:, tokens]
@@ -242,55 +242,60 @@ def tile_moe_shf_glu_sigmoid_kernel(
             nc.scalar.copy(ys[c][:, :rows, :], sums[:, :rows, :])
             return sums
 
-        def pick(n, c, terms):
-            entries = slice(c * GROUP // PER_COLUMN, (c + 1) * GROUP // PER_COLUMN)
-            gated = [terms[:, r * GROUP : (r + 1) * GROUP] for r in range(2)]
+        def pick(n, start, width, terms):
+            c, at = start // GROUP, start % GROUP
+            entries = slice(start // PER_COLUMN, (start + width) // PER_COLUMN)
+            gated = [terms[:, r * width : (r + 1) * width] for r in range(2)]
             for r, pos_sb in enumerate((pos1_sb, pos2_sb)):
-                nc.vector.tensor_tensor(gated[r], y[n][:].indirect(pos_sb[:, entries]), gate_sb[c][:, r, :], MULT)
+                nc.vector.tensor_tensor(gated[r], y[n][:].indirect(pos_sb[:, entries]), gate_sb[c][:, r, at : at + width], MULT)
             return gated
 
-        def add_across(n, c, gated):
-            terms = [ys[c][:, n, :]] + gated
-            across = w1_bank([P, H], "across%d%d" % (n, c))
-            for j in range(GROUP // P):
+        def add_turned(across, term, first, last):
+            blocks = across.shape[1] // P
+            for j in range(blocks):
                 cols = slice(j * P, (j + 1) * P)
-                for i, term in enumerate(terms):
-                    nc.tensor.matmul(across[:, cols], lhsT=term[:, cols], rhs=ident[:], is_transpose=True,
-                                     start=(i == 0), stop=(i == len(terms) - 1))
-            summed = held([P, GROUP], F32, "summed_%d_%d" % (n, c))
-            nc.scalar.copy(summed[:], across[:, :GROUP])
+                nc.tensor.matmul(across[:, cols], lhsT=term[:, cols], rhs=ident[:], is_transpose=True,
+                                 start=first and j == 0, stop=last and j == blocks - 1)
+
+        def open_across(n, start, width):
+            across = w1_bank([P, width], "across%d_%d" % (n, start))
+            add_turned(across, ys[start // GROUP][:, n, start % GROUP : start % GROUP + width], True, False)
+            return across
+
+        def close_across(n, start, width, across, gated, tag):
+            add_turned(across, gated[0], False, False)
+            add_turned(across, gated[1], False, True)
+            summed = held([P, width], F32, "summed%d_%d" % (n, start), tag)
+            nc.scalar.copy(summed[:], across[:])
             return summed
 
-        def turn_back(n, c, summed):
-            back = w3_bank([P, H], "back%d%d" % (n, c))
-            for j in range(GROUP // P):
+        def turn_back(n, start, width, summed):
+            back = w3_bank([P, width], "back%d_%d" % (n, start))
+            for j in range(width // P):
                 cols = slice(j * P, (j + 1) * P)
                 nc.tensor.transpose(back[:, cols], summed[:, cols], ident[:])
-            total = held([P, GROUP], F32, "total_%d_%d" % (n, c))
-            nc.scalar.copy(total[:], back[:, :GROUP])
-            nc.scalar.dma_start(out[n * P : (n + 1) * P, c * GROUP : (c + 1) * GROUP], total[:])
+            total = held([P, width], F32, "total%d_%d" % (n, start))
+            nc.scalar.copy(total[:], back[:])
+            nc.sync.dma_start(out[n * P : (n + 1) * P, start : start + width], total[:])
 
-        def add_shared(c, gated, shared_sums):
-            part = held([P, GROUP], F32, "part_%d" % c)
-            nc.vector.tensor_tensor(part[:], gated[0], shared_sums, ADD)
-            return part
+        def add_on_vector(n, start, width, gated, shared_sums):
+            part = held([P, width], F32, "part")
+            total = held([P, width], F32, "total", "before_last_adds")
+            halves = [slice(j * P, (j + 1) * P) for j in range(width // P)]
+            for cols in halves:
+                nc.vector.tensor_tensor(part[:, cols], gated[0][:, cols], shared_sums[:, cols], ADD)
+            for cols in halves:
+                nc.vector.tensor_tensor(total[:, cols], part[:, cols], gated[1][:, cols], ADD)
+            nc.sync.dma_start(out[n * P : (n + 1) * P, start : start + width], total[:])
 
-        def add_on_vector(n, c, gated, part):
-            total = held([P, GROUP], F32, "total_%d_%d" % (n, c))
-            nc.vector.tensor_tensor(total[:], part[:], gated[1], ADD)
-            nc.sync.dma_start(out[n * P : (n + 1) * P, c * GROUP : (c + 1) * GROUP], total[:])
-
-        idle = turn_bank([P, H], "idle")
-        for i in range(WARM_PASSES):
-            nc.tensor.matmul_mx(idle[:], lhsT=x_sb[:, :P].bitcast(FP8X4), lhsT_scale=x_plane[:, :P],
-                                rhs=x_sb[:, :H].bitcast(FP8X4), rhs_scale=x_plane[:, :H], start=True, stop=True)
-        gather_words(0, "words0")
-        gather_words(1, "words1")
+        gather_words(0, held([P, C], U32, "words0", "until_expert0")[:])
         gather_scales(0, 1)
-        gather_scales(1, 2)
+        gather_scales(1, 2, "until_expert1")
         gather_scales(2, 4)
         gather_scales(4, 6)
-        gather_words(2, "words2")
+        next_words = held([P, 2 * C], U32, "next_words", "until_expert2")
+        gather_words(1, next_words[:, :C])
+        gather_words(2, next_words[:, C:])
 
         halves = [(g, [half]) for g in range(E, GROUPS) for half in range(2)]
         gathers_end = E - GATHERED_AHEAD
@@ -304,7 +309,7 @@ def tile_moe_shf_glu_sigmoid_kernel(
             if step >= 2:
                 keep_sums(0, step - 2)
             sigmoid(step + 1 if step + 1 < E else GROUPS - 1)
-            if step == 0:
+            if step == 1:
                 for g, half in halves[EARLY_SIGMOIDS:4]:
                     sigmoid(g, half)
             if step >= gathers_end:
@@ -316,7 +321,7 @@ def tile_moe_shf_glu_sigmoid_kernel(
                 quantise(step - 1)
                 second_layer(0, [step - 1])
             if step < gathers_end:
-                gather_words(step + GATHERED_AHEAD, "words%d" % step)
+                gather_words(step + GATHERED_AHEAD, held([P, C], U32, "words%d" % (step + GATHERED_AHEAD), "until_expert%d" % step)[:])
             else:
                 product(*halves[step - gathers_end])
 
@@ -341,23 +346,29 @@ def tile_moe_shf_glu_sigmoid_kernel(
         turn(E + 2)
         interleave(E + 2)
 
-        pieces = [(n, c) for n in range(ROW_TILES) for c in range(TOKEN_GROUPS)]
-        shared_sums = [shared_second_layer(0, sum_bank, 2), shared_second_layer(1, w1_bank, 1)]
+        pieces = [(n, c * GROUP, GROUP) for n in range(ROW_TILES) for c in range(TOKEN_GROUPS)]
+        pieces[-2:-1] = [(1, GROUP, P), (1, GROUP + P, P)]
+        shared_second_layer(0, sum_bank, 2)
+        shared_second_layer(1, w1_bank, 2)
         for e in range(2, E, 2):
             second_layer(1, [e, e + 1], w3_bank)
             keep_sums(1, e)
-        gated = [pick(0, 0, held([P, 2 * GROUP], F32, "first_terms"))]
+        gated = [pick(*pieces[0], held([P, 2 * GROUP], F32, "first_terms"))]
         quantise(E + 2)
-        shared_sums.append(shared_second_layer(2, turn_bank, 1))
-        later_terms = held([P, 2 * GROUP * (len(pieces) - 1)], F32, "later_terms", "after_last_quantise")
-        for j, (n, c) in enumerate(pieces[1:]):
-            gated.append(pick(n, c, later_terms[:, 2 * j * GROUP : 2 * (j + 1) * GROUP]))
-        on_tensor = len(pieces) - VECTOR_PIECES
-        summed = [add_across(n, c, gated[j]) for j, (n, c) in enumerate(pieces[:1])]
-        for j in range(on_tensor):
-            if j + 1 < on_tensor:
-                summed.append(add_across(*pieces[j + 1], gated[j + 1]))
-            turn_back(*pieces[j], summed[j])
-        parts = [add_shared(c, gated[on_tensor + j], shared_sums[c][:, n, :]) for j, (n, c) in enumerate(pieces[on_tensor:])]
-        for j, (n, c) in enumerate(pieces[on_tensor:]):
-            add_on_vector(n, c, gated[on_tensor + j], parts[j])
+        last_sums = shared_second_layer(2, turn_bank, 1)
+        later_terms = held([P, 2 * (ROW_TILES * T - GROUP)], F32, "later_terms", "after_last_quantise")
+        at = 0
+        for n, start, width in pieces[1:]:
+            gated.append(pick(n, start, width, later_terms[:, at : at + 2 * width]))
+            at += 2 * width
+        on_tensor = len(pieces) - 1
+        across = [open_across(*piece) for piece in pieces[:2]]
+        summed = []
+        for j in range(on_tensor + 1):
+            if j < on_tensor:
+                summed.append(close_across(*pieces[j], across[j], gated[j], "before_last_adds" if j == on_tensor - 2 else None))
+            if j >= 1:
+                turn_back(*pieces[j - 1], summed[j - 1])
+            if j + 2 < on_tensor:
+                across.append(open_across(*pieces[j + 2]))
+        add_on_vector(*pieces[-1], gated[-1], last_sums[:, 1, :])

@@ -28,7 +28,6 @@ PER_COLUMN = 16
 FIRST_LOAD = 1
 SECOND_LOAD = 3
 GATHERED_AHEAD = 3
-EARLY_SIGMOIDS = 3
 
 
 def tile_moe_shf_glu_sigmoid_kernel(
@@ -76,7 +75,7 @@ def tile_moe_shf_glu_sigmoid_kernel(
         w1s_sb = held([P, 4 * H], U8, "w1s_sb")
         w3s_sb = held([P, 4 * H], U8, "w3s_sb")
         w2s_sb = held([P, 4 * N], U8, "w2s_sb")
-        gate_sb = [held([P, 2, GROUP], F32, "gate%d" % c) for c in range(TOKEN_GROUPS)]
+        gate_sb = [held([P, T], F32, "gate%d" % r) for r in range(2)]
         ident = held([P, P], F32, "ident")
         table_warm = held([P, 8], F32, "table_warm")
         y = [held([P, SLOTS], F32, "y%d" % n) for n in range(ROW_TILES)]
@@ -133,8 +132,8 @@ def tile_moe_shf_glu_sigmoid_kernel(
         nc.sync.dma_start(pos2_sb[:], pos2)
         load_plane(w2s_plane, w2s_scales)
         load_fp8(w2s_sb, w2s_words)
-        for c in range(TOKEN_GROUPS):
-            nc.sync.dma_start(gate_sb[c][:], gate.rearrange("r p t -> p r t")[:, :, c * GROUP : (c + 1) * GROUP])
+        for r in range(2):
+            nc.sync.dma_start(gate_sb[r][:], gate[r])
 
         slot_words = []
         slot_planes = []
@@ -170,11 +169,12 @@ def tile_moe_shf_glu_sigmoid_kernel(
         sums_ps = {}
         codes = {}
 
-        def sigmoid(g, halves=range(2)):
+        def sigmoid(g, halves=range(2), bank=w1_bank):
             for half in halves:
-                a = w1_bank([P, H], "a%d%d" % (g, half))
+                a = bank([P, H], "a%d%d" % (g, half))
                 first_product(a, g, half, (w1_sb, w1_plane), (w1s_sb, w1s_plane))
-                sig = work.tile([P, 2, P, 2], F32, name="sig%d%d" % (g, half), tag="sig" if g < E else "shared_sig", bufs=4 if g < E else 6)
+                tag, bufs = ("sig", 4) if g < E else ("shared_sig", 2 * TOKEN_GROUPS)
+                sig = work.tile([P, 2, P, 2], F32, name="sig%d%d" % (g, half), tag=tag, bufs=bufs)
                 nc.scalar.activation(sig[:], a[:].rearrange("s (q u e) -> s u q e", u=2, e=2), SIGMOID)
                 sigs[g, half] = sig
 
@@ -187,9 +187,11 @@ def tile_moe_shf_glu_sigmoid_kernel(
         def product(g, halves=range(2)):
             for half in halves:
                 if half == 0:
-                    hidden[g] = work.tile([P, 2, H], BF16, name="hh%d" % g, tag="h" if g < E else "shared_h", bufs=3, align_bytes=64)
+                    hidden[g] = work.tile([P, 2, H], BF16, name="hh%d" % g, tag="h" if g < E else "shared_h",
+                                          bufs=3, align_bytes=64)
                 nc.vector.tensor_tensor(hidden[g][:, half, :].rearrange("s (u q e) -> s u q e", u=2, e=2),
-                                        linear[g, half][:].rearrange("s (q u e) -> s u q e", u=2, e=2), sigs[g, half][:], MULT)
+                                        linear[g, half][:].rearrange("s (q u e) -> s u q e", u=2, e=2),
+                                        sigs[g, half][:], MULT)
 
         def turn(g, bank=turn_bank):
             turned = bank([P, 2, 2, P], "turned%d" % g)
@@ -242,13 +244,10 @@ def tile_moe_shf_glu_sigmoid_kernel(
             nc.scalar.copy(ys[c][:, :rows, :], sums[:, :rows, :])
             return sums
 
-        def pick(n, start, width, terms):
-            c, at = start // GROUP, start % GROUP
+        def pick(r, n, start, width, term):
             entries = slice(start // PER_COLUMN, (start + width) // PER_COLUMN)
-            gated = [terms[:, r * width : (r + 1) * width] for r in range(2)]
-            for r, pos_sb in enumerate((pos1_sb, pos2_sb)):
-                nc.vector.tensor_tensor(gated[r], y[n][:].indirect(pos_sb[:, entries]), gate_sb[c][:, r, at : at + width], MULT)
-            return gated
+            window = y[n][:].indirect((pos1_sb, pos2_sb)[r][:, entries])
+            nc.vector.tensor_tensor(term, window, gate_sb[r][:, start : start + width], MULT)
 
         def add_turned(across, term, first, last):
             blocks = across.shape[1] // P
@@ -289,39 +288,41 @@ def tile_moe_shf_glu_sigmoid_kernel(
             nc.sync.dma_start(out[n * P : (n + 1) * P, start : start + width], total[:])
 
         gather_words(0, held([P, C], U32, "words0", "until_expert0")[:])
-        gather_scales(0, 1)
-        gather_scales(1, 2, "until_expert1")
+        gather_scales(0, 2, "until_expert1")
         gather_scales(2, 4)
         gather_scales(4, 6)
-        next_words = held([P, 2 * C], U32, "next_words", "until_expert2")
-        gather_words(1, next_words[:, :C])
-        gather_words(2, next_words[:, C:])
+        next_words = held([P, (GATHERED_AHEAD - 1) * C], U32, "next_words", "until_expert2")
+        gather(x_sb, next_words[:], 1, GATHERED_AHEAD, slot_words)
 
         halves = [(g, [half]) for g in range(E, GROUPS) for half in range(2)]
         gathers_end = E - GATHERED_AHEAD
         sigmoid(0)
-        for g, half in halves[:EARLY_SIGMOIDS]:
-            sigmoid(g, half)
+        for (g, half), bank in zip(halves, (w1_bank, turn_bank, sum_bank, w1_bank)):
+            sigmoid(g, half, bank)
         w3_sums(0)
+
         for step in range(E):
             if step >= 1:
                 interleave(step - 1)
             if step >= 2:
                 keep_sums(0, step - 2)
             sigmoid(step + 1 if step + 1 < E else GROUPS - 1)
-            if step == 1:
-                for g, half in halves[EARLY_SIGMOIDS:4]:
-                    sigmoid(g, half)
             if step >= gathers_end:
                 w3_sums(*halves[step - gathers_end])
-            w3_sums(*((step + 1, range(2)) if step + 1 < E else halves[GATHERED_AHEAD]))
+            if step + 1 < E:
+                w3_sums(step + 1, [0] if step >= gathers_end else range(2))
+            else:
+                w3_sums(*halves[GATHERED_AHEAD])
             product(step)
             turn(step)
+            if gathers_end <= step < E - 1:
+                w3_sums(step + 1, [1])
             if step >= 1:
                 quantise(step - 1)
                 second_layer(0, [step - 1])
             if step < gathers_end:
-                gather_words(step + GATHERED_AHEAD, held([P, C], U32, "words%d" % (step + GATHERED_AHEAD), "until_expert%d" % step)[:])
+                e = step + GATHERED_AHEAD
+                gather_words(e, held([P, C], U32, "words%d" % e, "until_expert%d" % step)[:])
             else:
                 product(*halves[step - gathers_end])
 
@@ -353,20 +354,26 @@ def tile_moe_shf_glu_sigmoid_kernel(
         for e in range(2, E, 2):
             second_layer(1, [e, e + 1], w3_bank)
             keep_sums(1, e)
-        gated = [pick(*pieces[0], held([P, 2 * GROUP], F32, "first_terms"))]
+        first_terms = held([P, 2, GROUP], F32, "first_terms")
+        for r in range(2):
+            pick(r, *pieces[0], first_terms[:, r, :])
         quantise(E + 2)
         last_sums = shared_second_layer(2, turn_bank, 1)
-        later_terms = held([P, 2 * (ROW_TILES * T - GROUP)], F32, "later_terms", "after_last_quantise")
-        at = 0
+        later_terms = held([P, 2, ROW_TILES * T], F32, "later_terms", "after_last_quantise")
+        gated = [[first_terms[:, r, :] for r in range(2)]]
         for n, start, width in pieces[1:]:
-            gated.append(pick(n, start, width, later_terms[:, at : at + 2 * width]))
-            at += 2 * width
+            gated.append([later_terms[:, r, n * T + start : n * T + start + width] for r in range(2)])
+            wide = GROUP if n else T - GROUP
+            if (start - GROUP) % wide == 0:
+                pick(0, n, start, wide, later_terms[:, 0, n * T + start : n * T + start + wide])
+            pick(1, n, start, width, gated[-1][1])
         on_tensor = len(pieces) - 1
         across = [open_across(*piece) for piece in pieces[:2]]
         summed = []
         for j in range(on_tensor + 1):
             if j < on_tensor:
-                summed.append(close_across(*pieces[j], across[j], gated[j], "before_last_adds" if j == on_tensor - 2 else None))
+                tag = "before_last_adds" if j == on_tensor - 2 else None
+                summed.append(close_across(*pieces[j], across[j], gated[j], tag))
             if j >= 1:
                 turn_back(*pieces[j - 1], summed[j - 1])
             if j + 2 < on_tensor:

from contextlib import ExitStack

import concourse.mybir as mybir
from concourse.masks import make_identity

K, T, E, C, H, N = 512, 768, 6, 256, 512, 256
SLOTS = E * C
FLOPS = 2 * (SLOTS + T) * (2 * K * H + H * N)

F32 = mybir.dt.float32
BF16 = mybir.dt.bfloat16
I32 = mybir.dt.int32
U32 = mybir.dt.uint32
U16 = mybir.dt.uint16
U8 = mybir.dt.uint8
FP8X4 = mybir.dt.float8_e4m3fn_x4
FP4X4 = mybir.dt.float4_e2m1fn_x4
MULT = mybir.AluOpType.mult
ADD = mybir.AluOpType.add
SIGMOID = mybir.ActivationFunctionType.Sigmoid

P = 128
GROUP = 256
TOKEN_GROUPS = T // GROUP
GROUPS = E + TOKEN_GROUPS
ROW_TILES = N // P
PER_COLUMN = 16
FIRST_LOAD = 1
SECOND_LOAD = 3
GATHERED_AHEAD = 3


def tile_moe_shf_glu_sigmoid_kernel(
    tc, x_words, x_scales, w1_words, w1_scales, w3_words, w3_scales, w2_words, w2_scales,
    w1s_words, w1s_scales, w3s_words, w3s_scales, w2s_words, w2s_scales, gate, offs, pos1, pos2, out,
):
    nc = tc.nc
    with ExitStack() as ctx:
        keep = ctx.enter_context(tc.tile_pool(name="keep", bufs=1))
        work = ctx.enter_context(tc.tile_pool(name="work", bufs=4))
        psum = ctx.enter_context(tc.psum_pool(name="psum", bufs=1))

        def held(shape, dtype, name, tag=None):
            return keep.tile(shape, dtype, name=name, tag=tag or name, align_bytes=64)

        def w1_bank(shape, name):
            return psum.tile(shape, F32, name=name, tag="w1_bank", bufs=3)

        def w3_bank(shape, name):
            return psum.tile(shape, F32, name=name, tag="w3_bank", bufs=3)

        def turn_bank(shape, name):
            return psum.tile(shape, F32, name=name, tag="turn_bank", bufs=1)

        def sum_bank(shape, name):
            return psum.tile(shape, F32, name=name, tag="sum_bank", bufs=1)

        offs_sb = keep.tile([P, SLOTS // PER_COLUMN], U16, name="offs_sb")
        pos1_sb = keep.tile([P, T // PER_COLUMN], U16, name="pos1_sb")
        pos2_sb = keep.tile([P, T // PER_COLUMN], U16, name="pos2_sb")
        x_sb = held([P, T], U32, "x_sb")
        x_plane = held([P, T], U8, "x_plane")
        w1_first = held([P, FIRST_LOAD, 2 * H], U8, "w1_first", "until_expert2")
        w1_rest = held([P, E - FIRST_LOAD, 2 * H], U8, "w1_rest")
        w1_sb = [w1_first[:, e, :] for e in range(FIRST_LOAD)] + [w1_rest[:, e, :] for e in range(E - FIRST_LOAD)]
        w3_all = held([P, E, 2 * H], U8, "w3_all")
        w3_sb = [w3_all[:, e, :] for e in range(E)]
        w2_sb = held([P, E, 2 * N], U8, "w2_sb")
        w1_plane = held([P, E * H], U8, "w1_plane")
        w3_plane = held([P, E * H], U8, "w3_plane")
        w2_plane = held([P, E * N], U8, "w2_plane")
        w1s_plane = held([P, H], U8, "w1s_plane")
        w3s_plane = held([P, H], U8, "w3s_plane")
        w2s_plane = held([P, N], U8, "w2s_plane")
        w1s_sb = held([P, 4 * H], U8, "w1s_sb")
        w3s_sb = held([P, 4 * H], U8, "w3s_sb")
        w2s_sb = held([P, 4 * N], U8, "w2s_sb")
        gate_sb = [held([P, T], F32, "gate%d" % r) for r in range(2)]
        ident = held([P, P], F32, "ident")
        table_warm = held([P, 8], F32, "table_warm")
        y = [held([P, SLOTS], F32, "y%d" % n) for n in range(ROW_TILES)]
        ys = [held([P, ROW_TILES, GROUP], F32, "ys%d" % c) for c in range(TOKEN_GROUPS)]

        def zero(engine, plane):
            engine.memset(plane[:].bitcast(I32), 0)

        def load_plane(plane, scales, queue=nc.sync):
            for r in range(4):
                rows = scales.rearrange("m (q r) c -> r q m c", r=4)
                dst = plane[r:P:32, :].bitcast(I32).rearrange("q (m c) -> q m c", m=scales.shape[0])
                queue.dma_start(dst, rows[r].bitcast(I32))

        def load_fp4(dst, words, lo, hi):
            src = words.rearrange("e s p b -> p (e s) b")
            nc.sync.dma_start(dst.bitcast(I32), src[:, lo:hi, :].bitcast(I32))

        def load_fp8(dst, words):
            nc.sync.dma_start(dst[:].bitcast(I32), words[0].rearrange("p c d -> p (c d)").bitcast(I32))

        def by_matrix(scales):
            return scales.rearrange("e s b c -> (e s) b c")

        zero(nc.gpsimd, x_plane)
        zero(nc.vector, w1_plane)
        zero(nc.vector, w1s_plane)
        nc.vector.memset(table_warm[:], 0.0)
        nc.scalar.activation(table_warm[:], table_warm[:], SIGMOID)
        zero(nc.vector, w3_plane)
        make_identity(nc, ident[:])
        zero(nc.gpsimd, w2_plane)
        zero(nc.vector, w3s_plane)
        zero(nc.vector, w2s_plane)
        load_plane(w2_plane, by_matrix(w2_scales), nc.gpsimd)
        load_plane(w3s_plane, w3s_scales, nc.gpsimd)

        load_fp8(x_sb, x_words)
        nc.sync.dma_start(offs_sb[:], offs)
        load_plane(x_plane, x_scales)
        load_fp4(w1_first[:], w1_words, 0, FIRST_LOAD)
        load_plane(w1_plane, by_matrix(w1_scales))
        load_plane(w1s_plane, w1s_scales)
        load_fp8(w1s_sb, w1s_words)
        load_fp4(w3_all[:, :FIRST_LOAD, :], w3_words, 0, FIRST_LOAD)
        load_plane(w3_plane, by_matrix(w3_scales))
        load_fp4(w1_rest[:, : SECOND_LOAD - FIRST_LOAD, :], w1_words, FIRST_LOAD, SECOND_LOAD)
        load_fp4(w3_all[:, FIRST_LOAD:SECOND_LOAD, :], w3_words, FIRST_LOAD, SECOND_LOAD)
        load_fp4(w2_sb[:], w2_words, 0, E)
        load_fp4(w1_rest[:, SECOND_LOAD - FIRST_LOAD :, :], w1_words, SECOND_LOAD, E)
        load_fp4(w3_all[:, SECOND_LOAD:, :], w3_words, SECOND_LOAD, E)
        load_fp8(w3s_sb, w3s_words)
        nc.sync.dma_start(pos1_sb[:], pos1)
        nc.sync.dma_start(pos2_sb[:], pos2)
        load_plane(w2s_plane, w2s_scales)
        load_fp8(w2s_sb, w2s_words)
        for r in range(2):
            nc.sync.dma_start(gate_sb[r][:], gate[r])

        slot_words = []
        slot_planes = []

        def gather(source, gathered, lo, hi, into):
            entries = offs_sb[:, lo * C // PER_COLUMN : hi * C // PER_COLUMN]
            nc.vector.tensor_copy(gathered, source[:].indirect(entries))
            into.extend(gathered[:, e * C : (e + 1) * C] for e in range(hi - lo))

        def gather_words(e, gathered):
            gather(x_sb, gathered, e, e + 1, slot_words)

        def gather_scales(lo, hi, tag=None):
            gather(x_plane, held([P, (hi - lo) * C], U8, "scales%d" % lo, tag)[:], lo, hi, slot_planes)

        def first_product(acc, g, half, routed, shared):
            cols = slice(half * P, (half + 1) * P)
            if g < E:
                words, plane = slot_words[g], slot_planes[g]
                w, w_plane = routed[0][g].bitcast(FP4X4), routed[1][:, g * H : (g + 1) * H]
            else:
                tokens = slice((g - E) * GROUP, (g - E + 1) * GROUP)
                words, plane = x_sb[:, tokens], x_plane[:, tokens]
                w, w_plane = shared[0][:].bitcast(FP8X4), shared[1][:]
            nc.tensor.matmul_mx(acc[:], lhsT=words[:, cols].bitcast(FP8X4), lhsT_scale=plane[:, cols],
                                rhs=w, rhs_scale=w_plane, start=True, stop=True)

        sigs = {}
        hidden = {}
        linear = {}
        turned_ps = {}
        turned_sb = {}
        sums_ps = {}
        codes = {}

        def sigmoid(g, halves=range(2), bank=w1_bank):
            for half in halves:
                a = bank([P, H], "a%d%d" % (g, half))
                first_product(a, g, half, (w1_sb, w1_plane), (w1s_sb, w1s_plane))
                tag, bufs = ("sig", 4) if g < E else ("shared_sig", 2 * TOKEN_GROUPS)
                sig = work.tile([P, 2, P, 2], F32, name="sig%d%d" % (g, half), tag=tag, bufs=bufs)
                nc.scalar.activation(sig[:], a[:].rearrange("s (q u e) -> s u q e", u=2, e=2), SIGMOID)
                sigs[g, half] = sig

        def w3_sums(g, halves=range(2)):
            for half in halves:
                b = w3_bank([P, H], "b%d%d" % (g, half))
                first_product(b, g, half, (w3_sb, w3_plane), (w3s_sb, w3s_plane))
                linear[g, half] = b

        def product(g, halves=range(2)):
            for half in halves:
                if half == 0:
                    hidden[g] = work.tile([P, 2, H], BF16, name="hh%d" % g, tag="h" if g < E else "shared_h",
                                          bufs=3, align_bytes=64)
                nc.vector.tensor_tensor(hidden[g][:, half, :].rearrange("s (u q e) -> s u q e", u=2, e=2),
                                        linear[g, half][:].rearrange("s (q u e) -> s u q e", u=2, e=2),
                                        sigs[g, half][:], MULT)

        def turn(g, bank=turn_bank):
            turned = bank([P, 2, 2, P], "turned%d" % g)
            for half in range(2):
                pairs = hidden[g][:, half, :].bitcast(F32)
                for u in range(2):
                    nc.tensor.transpose(turned[:, half, u, :], pairs[:, u * P : (u + 1) * P], ident[:])
            turned_ps[g] = turned

        def interleave(g):
            if g < GROUPS - 1:
                grouped = work.tile([P, 2 * GROUP], F32, name="grouped%d" % g, tag="grouped", align_bytes=64)
            else:
                grouped = held([P, 2 * GROUP], F32, "grouped%d" % g, "after_last_quantise")
            nc.scalar.copy(grouped[:].rearrange("p (h s u) -> p h s u", h=2, u=2),
                           turned_ps[g][:].rearrange("p h u s -> p h s u"))
            turned_sb[g] = grouped

        def quantise(g):
            h_words = work.tile([P, GROUP], U32, name="h_words%d" % g, tag="h_words", bufs=GROUPS, align_bytes=64)
            h_plane = work.tile([P, GROUP], U8, name="h_plane%d" % g, tag="h_plane", bufs=GROUPS, align_bytes=64)
            nc.vector.quantize_mx(out=h_words[:].bitcast(FP8X4), scales=h_plane[:], in_=turned_sb[g][:].bitcast(BF16))
            codes[g] = h_words, h_plane

        def second_product(g, n, acc):
            h_words, h_plane = codes[g]
            if g < E:
                w = w2_sb[:, g, 2 * n * P : 2 * (n + 1) * P].bitcast(FP4X4)
                w_plane = w2_plane[:, g * N + n * P : g * N + (n + 1) * P]
            else:
                w = w2s_sb[:, 4 * n * P : 4 * (n + 1) * P].bitcast(FP8X4)
                w_plane = w2s_plane[:, n * P : (n + 1) * P]
            nc.tensor.matmul_mx(acc, lhsT=w, lhsT_scale=w_plane, rhs=h_words[:].bitcast(FP8X4),
                                rhs_scale=h_plane[:], start=True, stop=True)

        def second_layer(n, groups, bank=sum_bank):
            sums = bank([P, len(groups) * GROUP], "sums%d_%d" % (n, groups[0]))
            for j, g in enumerate(groups):
                second_product(g, n, sums[:, j * GROUP : (j + 1) * GROUP])
            sums_ps[n, groups[0]] = sums

        def keep_sums(n, g):
            sums = sums_ps[n, g]
            nc.scalar.copy(y[n][:, g * GROUP : g * GROUP + sums.shape[1]], sums[:])

        def shared_second_layer(c, bank, rows):
            sums = bank([P, ROW_TILES, GROUP], "shared_sums%d" % c)
            for n in range(ROW_TILES):
                second_product(E + c, n, sums[:, n, :])
            nc.scalar.copy(ys[c][:, :rows, :], sums[:, :rows, :])
            return sums

        def pick(r, n, start, width, term):
            entries = slice(start // PER_COLUMN, (start + width) // PER_COLUMN)
            window = y[n][:].indirect((pos1_sb, pos2_sb)[r][:, entries])
            nc.vector.tensor_tensor(term, window, gate_sb[r][:, start : start + width], MULT)

        def add_turned(across, term, first, last):
            blocks = across.shape[1] // P
            for j in range(blocks):
                cols = slice(j * P, (j + 1) * P)
                nc.tensor.matmul(across[:, cols], lhsT=term[:, cols], rhs=ident[:], is_transpose=True,
                                 start=first and j == 0, stop=last and j == blocks - 1)

        def open_across(n, start, width):
            across = w1_bank([P, width], "across%d_%d" % (n, start))
            add_turned(across, ys[start // GROUP][:, n, start % GROUP : start % GROUP + width], True, False)
            return across

        def close_across(n, start, width, across, gated, tag):
            add_turned(across, gated[0], False, False)
            add_turned(across, gated[1], False, True)
            summed = held([P, width], F32, "summed%d_%d" % (n, start), tag)
            nc.scalar.copy(summed[:], across[:])
            return summed

        def turn_back(n, start, width, summed):
            back = w3_bank([P, width], "back%d_%d" % (n, start))
            for j in range(width // P):
                cols = slice(j * P, (j + 1) * P)
                nc.tensor.transpose(back[:, cols], summed[:, cols], ident[:])
            total = held([P, width], F32, "total%d_%d" % (n, start))
            nc.scalar.copy(total[:], back[:])
            nc.sync.dma_start(out[n * P : (n + 1) * P, start : start + width], total[:])

        def add_on_vector(n, start, width, gated, shared_sums):
            part = held([P, width], F32, "part")
            total = held([P, width], F32, "total", "before_last_adds")
            halves = [slice(j * P, (j + 1) * P) for j in range(width // P)]
            for cols in halves:
                nc.vector.tensor_tensor(part[:, cols], gated[0][:, cols], shared_sums[:, cols], ADD)
            for cols in halves:
                nc.vector.tensor_tensor(total[:, cols], part[:, cols], gated[1][:, cols], ADD)
            nc.sync.dma_start(out[n * P : (n + 1) * P, start : start + width], total[:])

        gather_words(0, held([P, C], U32, "words0", "until_expert0")[:])
        gather_scales(0, 2, "until_expert1")
        gather_scales(2, 4)
        gather_scales(4, 6)
        next_words = held([P, (GATHERED_AHEAD - 1) * C], U32, "next_words", "until_expert2")
        gather(x_sb, next_words[:], 1, GATHERED_AHEAD, slot_words)

        halves = [(g, [half]) for g in range(E, GROUPS) for half in range(2)]
        gathers_end = E - GATHERED_AHEAD
        sigmoid(0)
        for (g, half), bank in zip(halves, (w1_bank, turn_bank, sum_bank, w1_bank)):
            sigmoid(g, half, bank)
        w3_sums(0)

        for step in range(E):
            if step >= 1:
                interleave(step - 1)
            if step >= 2:
                keep_sums(0, step - 2)
            sigmoid(step + 1 if step + 1 < E else GROUPS - 1)
            if step >= gathers_end:
                w3_sums(*halves[step - gathers_end])
            if step + 1 < E:
                w3_sums(step + 1, [0] if step >= gathers_end else range(2))
            else:
                w3_sums(*halves[GATHERED_AHEAD])
            product(step)
            turn(step)
            if gathers_end <= step < E - 1:
                w3_sums(step + 1, [1])
            if step >= 1:
                quantise(step - 1)
                second_layer(0, [step - 1])
            if step < gathers_end:
                e = step + GATHERED_AHEAD
                gather_words(e, held([P, C], U32, "words%d" % e, "until_expert%d" % step)[:])
            else:
                product(*halves[step - gathers_end])

        last = E - 1
        interleave(last)
        keep_sums(0, last - 1)
        w3_sums(E + 2)
        product(E + 1, [1])
        product(E + 2, [0])
        turn(E, w1_bank)
        interleave(E)
        quantise(last)
        turn(E + 1, w1_bank)
        interleave(E + 1)
        second_layer(0, [last])
        keep_sums(0, last)
        product(E + 2, [1])
        quantise(E)
        quantise(E + 1)
        second_layer(1, [0, 1], w3_bank)
        keep_sums(1, 0)
        turn(E + 2)
        interleave(E + 2)

        pieces = [(n, c * GROUP, GROUP) for n in range(ROW_TILES) for c in range(TOKEN_GROUPS)]
        pieces[-2:-1] = [(1, GROUP, P), (1, GROUP + P, P)]
        shared_second_layer(0, sum_bank, 2)
        shared_second_layer(1, w1_bank, 2)
        for e in range(2, E, 2):
            second_layer(1, [e, e + 1], w3_bank)
            keep_sums(1, e)
        first_terms = held([P, 2, GROUP], F32, "first_terms")
        for r in range(2):
            pick(r, *pieces[0], first_terms[:, r, :])
        quantise(E + 2)
        last_sums = shared_second_layer(2, turn_bank, 1)
        later_terms = held([P, 2, ROW_TILES * T], F32, "later_terms", "after_last_quantise")
        gated = [[first_terms[:, r, :] for r in range(2)]]
        for n, start, width in pieces[1:]:
            gated.append([later_terms[:, r, n * T + start : n * T + start + width] for r in range(2)])
            wide = GROUP if n else T - GROUP
            if (start - GROUP) % wide == 0:
                pick(0, n, start, wide, later_terms[:, 0, n * T + start : n * T + start + wide])
            pick(1, n, start, width, gated[-1][1])
        on_tensor = len(pieces) - 1
        across = [open_across(*piece) for piece in pieces[:2]]
        summed = []
        for j in range(on_tensor + 1):
            if j < on_tensor:
                tag = "before_last_adds" if j == on_tensor - 2 else None
                summed.append(close_across(*pieces[j], across[j], gated[j], tag))
            if j >= 1:
                turn_back(*pieces[j - 1], summed[j - 1])
            if j + 2 < on_tensor:
                across.append(open_across(*pieces[j + 2]))
        add_on_vector(*pieces[-1], gated[-1], last_sums[:, 1, :])
